import numpy as np, ml_dtypes
CORES = [13,21,141,149]
N = 4
BF = ml_dtypes.bfloat16
def gentries(a):
    return np.ascontiguousarray(a.reshape(8, 16, -1).transpose(0, 2, 1)).reshape(8, -1)
def gtable(e):
    e = np.asarray(e); return np.ascontiguousarray(e.reshape(8, -1, 16).transpose(0, 2, 1)).reshape(128, -1).astype(np.int32)
M, L, S, ST = 512, 3, 1024, 6
LPR, C, W = 4, 1604, 6432
LEV = [(16, LPR, 0), (32, 16 * LPR, LPR)] + [(288 + d * N * M, M, 17 * LPR + d * M) for d in range(L)]
START = np.array([v[0] for v in LEV]); SIZE = np.array([v[1] for v in LEV])
A8 = np.arange(8)[:, None]
def grow(rng, bias):
    tri = np.zeros((N, 8, 16, C), np.int64); par = np.zeros((N, 8, C - LPR), np.int64); let = np.zeros((N, 8, C - LPR), np.int64)
    G = np.zeros((8, 16, W), np.int64); G[:, :, 0] = 16 + np.arange(16)
    D = [np.repeat(G[:, :, :1], LPR, axis=2) for r in range(N)]
    for d in range(len(LEV)):
        b, m, o = LEV[d]; new = []
        for r in range(N):
            own = tri[r, :, :, o:o + m]
            if d + 1 < len(LEV):
                b2, m2, o2 = LEV[d + 1]
                n = D[r].transpose(0, 2, 1); lev = np.searchsorted(START, n, side="right"); who = (n - START[lev - 1]) // SIZE[lev - 1]
                key = rng.random((8, m, 16)) + bias(d, r, lev, who)
                pick = rng.permuted(np.argsort(key.reshape(8, -1), axis=1)[:, :m2], axis=1)
                p = pick >> 4; c = pick & 15
                par[r, :, o2 - LPR:o2 - LPR + m2] = p; let[r, :, o2 - LPR:o2 - LPR + m2] = c
                own[A8, c, p] = b2 + r * m2 + np.arange(m2)
                new.append(D[r][A8, c, p])
            G[:, :, b + r * m:b + (r + 1) * m] = np.where(own != 0, own, D[r])
        D = [np.take_along_axis(G, fl[:, None, :], 2) for fl in new]
    return tri, par, let, G
def walk(rng, G, go):
    txt = np.zeros((N, 8, ST, S), np.int64); s = np.zeros((N, 8, S), np.int64)
    for t in range(ST):
        col = G[np.arange(8)[None, :, None], :, s]
        c = np.argmax(rng.random(col.shape) + (col > s[..., None]) * (rng.random((N, 8, S, 1)) < go[..., None]), axis=-1)
        txt[:, :, t] = c; s = np.take_along_axis(col, c[..., None], 3)[..., 0]
    return txt
def pack(tri, par, let, txt):
    return {"tri": np.ascontiguousarray(tri.reshape(N, 128, C)).astype(np.int32), "par": np.stack([gtable(a) for a in par]),
            "let": let.astype(np.int32), "txt": np.ascontiguousarray(txt.reshape(N, 8, ST * S)).astype(np.int32)}
def setup_inputs(rng):
    pull = rng.choice(np.array([0.0, 0.2, 0.5, 2.0]), (N, 8, 1, 1))
    tri, par, let, G = grow(rng, lambda d, r, lev, who: -pull[r] * lev)
    return pack(tri, par, let, walk(rng, G, rng.choice(np.array([0.3, 0.7, 0.95]), (N, 8, S))))
def setup_inputs_depth(rng):
    pull = np.where(rng.permutation(8) < 4, 4.0, -4.0).reshape(8, 1, 1)
    tri, par, let, G = grow(rng, lambda d, r, lev, who: -pull * lev)
    return pack(tri, par, let, walk(rng, G, rng.choice(np.array([0.5, 1.0, 1.0]), (N, 8, S))))
def setup_inputs_bushy(rng):
    def bias(d, r, lev, who):
        v = np.zeros(lev.shape); m = lev.shape[1]
        v[0::2] = 10.0 * np.argsort(rng.random((4, m)), axis=1)[:, :, None]
        v[1::2] = 10.0 * np.argsort(rng.random((4, m, 16)), axis=2)
        return v
    tri, par, let, G = grow(rng, bias)
    txt = walk(rng, G, rng.choice(np.array([0.2, 0.8, 1.0]), (N, 8, S)))
    for r in range(N):
        g = 2 * rng.permutation(4) + 1
        txt[r, g[0]] = (np.add.accumulate(rng.integers(1, 16, ST)) & 15)[:, None]
        txt[r, g[1]] = LPR * ((r + 1 + int(rng.integers(0, N - 1))) % N) + rng.integers(0, LPR, (ST, S))
    return pack(tri, par, let, txt)
def setup_inputs_ends(rng):
    def bias(d, r, lev, who):
        v = np.zeros(lev.shape); m = lev.shape[1]; p = np.arange(m); c = np.arange(16)
        v[0::2] = 100.0 * np.minimum(p, m - 1 - p)[None, :, None]
        v[1::2] = 10.0 * ((c != 0) & (c != 15))[None, None, :] - 0.5 * lev[1::2]
        return v
    tri, par, let, G = grow(rng, bias)
    txt = walk(rng, G, rng.choice(np.array([0.3, 0.7, 1.0]), (N, 8, S))); q = S >> 3
    txt[..., :q] = 0; txt[..., q:2 * q] = 15
    txt[..., 2 * q:3 * q] = (15 * (np.arange(ST) & 1))[None, None, :, None]
    txt[..., 3 * q:4 * q] = rng.integers(0, 16, (N, 8, 1, q)); txt[..., 4 * q:5 * q] = txt[..., 7 * q:7 * q + 1]
    return pack(tri, par, let, txt)
def setup_inputs_spread(rng):
    wt = np.stack([0.15 * rng.permutation(16) ** np.exp2(rng.integers(-1, 2)) for g in range(8)])[:, None, :]
    pull = rng.choice(np.array([-0.5, 0.0, 0.5, 3.0]), (len(LEV), N, 8, 1, 1)); q = int(rng.integers(0, N))
    tri, par, let, G = grow(rng, lambda d, r, lev, who: wt - pull[d, r] * lev + (100.0 if d == 2 else 0.0) * (who != q))
    txt = walk(rng, G, rng.random((N, 8, S)))
    odd = np.minimum((16 * rng.random((N, 8, ST, S)) ** np.exp2(rng.integers(-3, 4, (N, 8, 1, S)))).astype(np.int64), 15)
    return pack(tri, par, let, np.where(rng.random((N, 8, 1, S)) < 0.4, odd, txt))
def check_inputs(d):
    bad = []
    for k in ("let", "txt"):
        if np.min(d[k]) < 0 or np.max(d[k]) > 15: bad.append("range of " + k)
    par = np.stack([gentries(a) for a in d["par"]]).astype(np.int64); let = d["let"].astype(np.int64)
    for i in range(1, len(LEV)):
        m, o = LEV[i][1:]; part = par[:, :, o - LPR:o - LPR + m]
        if np.min(part) < 0 or np.max(part) >= LEV[i - 1][1]: bad.append("range of par on level " + str(i + 1))
    if bad: return bad
    want = np.zeros((N, 8, 16, C), np.int64)
    for i in range(1, len(LEV)):
        b, m, o = LEV[i]
        for r in range(N):
            want[r][A8, let[r, :, o - LPR:o - LPR + m], LEV[i - 1][2] + par[r, :, o - LPR:o - LPR + m]] = b + r * m + np.arange(m)
    if np.count_nonzero(want) != N * 8 * (C - LPR): bad.append("two states with one parent and letter")
    if not np.array_equal(want.reshape(N, 128, C), d["tri"]): bad.append("tri against par and let")
    return bad
def reference(tri, par, let, txt):
    t4 = tri.astype(np.int64).reshape(N, 8, 16, C); pl = np.stack([gentries(a) for a in par]).astype(np.int64)
    ll = let.astype(np.int64); tx = txt.astype(np.int64).reshape(N, 8, ST, S)
    G = np.zeros((8, 16, W), np.int64); G[:, :, 0] = 16 + np.arange(16)
    fail = np.zeros((8, W), np.int64)
    yg = np.zeros((N, 8, 16, C), np.int64); yf = np.zeros((N, 8, C), np.int64)
    for i in range(len(LEV)):
        b, m, o = LEV[i]
        for r in range(N):
            fl = np.zeros((8, m), np.int64)
            if i > 0:
                pb, pm = LEV[i - 1][:2]
                fp = np.take_along_axis(fail, pb + r * pm + pl[r, :, o - LPR:o - LPR + m], 1)
                fl = G[A8, ll[r, :, o - LPR:o - LPR + m], fp]
            own = t4[r, :, :, o:o + m]
            full = np.where(own != 0, own, np.take_along_axis(G, fl[:, None, :], 2))
            fail[:, b + r * m:b + (r + 1) * m] = fl; G[:, :, b + r * m:b + (r + 1) * m] = full
            yf[r, :, o:o + m] = fl; yg[r, :, :, o:o + m] = full
    s = np.zeros((N, 8, S), np.int64); big = np.zeros((N, 8, S), np.int64)
    for t in range(ST):
        s = G[np.arange(8)[None, :, None], tx[:, :, t], s]
        big = np.maximum(big, s)
    return {"yg": yg.reshape(N, 128, C).astype(np.float32), "yf": yf.astype(np.float32), "yl": s.astype(np.float32), "ym": big.astype(np.float32)}

@@ -1,0 +1,400 @@
+from concourse.bass import DstId, RemoteDMATransfer
+from concourse.mybir import AluOpType as A, ActivationFunctionType as AF
+
+SH = 4384
+S2 = 1184
+WS, WB, NB, WF = 68, 552, 548, 32
+G3, G4, GE = 256, 2304, 4352
+
+SCRATCH = {
+    "t12": ("sbuf", [128, 72], "int32"), "t3": ("sbuf", [128, 512], "int32"), "t4": ("sbuf", [128, 512], "int32"),
+    "pr": ("sbuf", [128, 100], "int32"), "pru": ("sbuf", [128, 100], "uint16"),
+    "lt": ("sbuf", [128, 2, 3, 16], "int32"), "lt2": ("sbuf", [128, 3, 32], "int32"),
+    "lt3": ("sbuf", [128, 96], "int32"), "ltu": ("sbuf", [128, 96], "uint16"),
+    "tx": ("sbuf", [128, 384], "int32"), "txu": ("sbuf", [128, 256], "uint16"),
+    "ta": ("sbuf", [128, 64], "float32"), "tb": ("sbuf", [128, 64], "float32"), "i01": ("sbuf", [128, 64], "uint16"),
+    "cst": ("sbuf", [128, 64], "bfloat16"), "dm": ("sbuf", [128, 128], "int32"), "p4": ("sbuf", [128, 4], "int32"),
+    "io": ("sbuf", [128, 256], "bfloat16"),
+    "sh8": ("sbuf", [128, 8], "int32"), "t16": ("sbuf", [128, 16], "int32"), "i16": ("sbuf", [128, 16], "bfloat16"),
+    "zb": ("sbuf", [128, 144], "bfloat16"), "zh": ("sbuf", [128, 144], "float16"), "zf": ("sbuf", [128, 144], "float32"),
+    "ih": ("sbuf", [128, 128], "float16"),
+    "ca": ("sbuf", [128, 4], "int32"), "cl": ("sbuf", [128, 4], "uint16"), "g1": ("sbuf", [128, 16], "float32"),
+    "l1": ("sbuf", [128, 4], "uint16"), "l1a": ("sbuf", [128, 16], "uint16"), "a16": ("sbuf", [128, 4], "float32"),
+    "lb3": ("sbuf", [128, 512], "bfloat16"), "x3": ("sbuf", [128, 576], "bfloat16"), "x4i": ("sbuf", [128, 512], "bfloat16"),
+    "i4": ("sbuf", [128, 32], "uint16"),
+    "m4": ("sbuf", [128, 512], "bfloat16"), "m5": ("sbuf", [128, 512], "bfloat16"), "mt": ("sbuf", [128, 4096], "bfloat16"),
+    "sS": ("sbuf", [128, 4, WS], "float32"), "sB3": ("sbuf", [128, 4 * WB], "float16"),
+    "sB4": ("sbuf", [128, 2048], "float16"), "sF": ("sbuf", [128, 4 * WF], "uint16"),
+    "lst": ("sbuf", [128, 144], "uint16"),
+    "w2": ("sbuf", [128, 256], "float32"), "wg": ("sbuf", [128, GE], "float32"), "n2": ("sbuf", [128, 256], "bfloat16"),
+    "xf4": ("sbuf", [128, 512], "float16"), "xh": ("sbuf", [128, 1024], "float16"), "xa": ("sbuf", [128, 1024], "float32"),
+    "xb": ("sbuf", [128, 512], "float32"), "xc": ("sbuf", [128, 1024], "float32"), "xs": ("sbuf", [128, 1024], "bfloat16"),
+    "i3": ("sbuf", [128, 64], "uint16"), "i4g": ("sbuf", [128, 64], "uint16"),
+    "i5": ("sbuf", [128, 64], "uint16"), "if5": ("sbuf", [128, 32], "uint16"),
+    "uc": ("sbuf", [128, 64], "float32"), "va": ("sbuf", [128, 64], "float32"), "vb": ("sbuf", [128, 64], "float32"),
+    "mx": ("sbuf", [128, 64], "float32"), "oyl": ("sbuf", [128, 64], "float32"), "oym": ("sbuf", [128, 64], "float32"),
+    "fl": ("sbuf", [128, 64], "float32"), "ft": ("sbuf", [128, 64], "float32"),
+    "oyg": ("sbuf", [128, 1604], "float32"), "of12": ("sbuf", [128, 68], "float32"), "of3": ("sbuf", [128, 512], "float32"),
+    "pt0": ("psum", [128, 512], "float32"), "pt1": ("psum", [128, 512], "float32"),
+    "pt2": ("psum", [128, 512], "float32"), "pt3": ("psum", [128, 512], "float32"),
+    "pl0": ("psum", [128, 512], "float32"), "pl1": ("psum", [128, 512], "float32"),
+    "pl2": ("psum", [128, 512], "float32"), "pl3": ("psum", [128, 512], "float32"),
+}
+SEMAPHORES = (["cv", "ca", "cp", "cg", "l12", "lpr", "llt", "lt3", "lt4", "ltx", "out", "snd", "aS"]
+              + ["a%s%d" % (k, q) for k in ("B3", "B4", "F") for q in range(4)])
+CARRIES = (("S", "B3", "F"), ("B4",))
+
+
+def routes(T, topo, rank):
+    core = T.cores[rank]
+    others = [q for q in range(len(T.cores)) if q != rank]
+    direct = [q for q in others if topo.may_write(core, T.cores[q])]
+    cross = [q for q in others if q not in direct]
+    cross.sort(key=lambda q: topo.host(T.cores[q]) != topo.host(core))
+    pairs = []
+    for k, q in enumerate(cross):
+        able = [h for h in topo.cores_of(core) if h != core and topo.may_write(h, T.cores[q])
+                and (topo.die(h) == topo.die(core)) == (k == 0)]
+        pairs.append((able, q))
+    return direct[0], pairs
+
+
+def slot(T, kind, q):
+    if kind == "S":
+        return T.sS[:, q, :]
+    w, n = {"B3": (WB, NB), "B4": (512, 512), "F": (WF, WF)}[kind]
+    return T["s" + kind][:, w * q:w * q + n]
+
+
+def asem(T, kind, q):
+    return T.sem["aS"] if kind == "S" else T.sem["a%s%d" % (kind, q)]
+
+
+def bits(engs):
+    return sum(1 << e for e in engs)
+
+
+def split(topo, core, T, rank):
+    d, pairs = routes(T, topo, rank)
+    off = topo.engines(core, T.cores[d])
+    on = [e for e in topo.engines(core, pairs[0][0][0]) if e not in off]
+    return on, off
+
+
+def helper_program(g, core, T, topo, rank, k, kinds):
+    d, pairs = routes(T, topo, rank)
+    n_in = len(split(topo, T.cores[rank], T, rank)[k])
+    dst = T.cores[pairs[k][1]]
+    rid, pid = topo.addr(dst, core)
+    sent = 0
+    for kind in kinds:
+        g.wait_ge(asem(T, kind, rank), n_in)
+        g.remote_dma(slot(T, kind, rank), slot(T, kind, rank), asem(T, kind, rank), T.sem.snd, pid, rid,
+                     topo.mask(core, dst))
+        sent += len(topo.engines(core, dst))
+    g.wait_ge(T.sem.snd, sent)
+
+
+def rank_program(g, core, T, topo):
+    r = T.rank_of(core)
+    if r is None:
+        for q in range(len(T.cores)):
+            for k, (able, _d) in enumerate(routes(T, topo, q)[1]):
+                for j, kinds in enumerate(CARRIES):
+                    if able[j] == core:
+                        helper_program(g, core, T, topo, q, k, kinds)
+        return
+
+    direct, pairs = routes(T, topo, r)
+    on, off = split(topo, core, T, r)
+    c1, c2 = pairs[0][1], pairs[1][1]
+    order = [r, direct, c1, c2]
+    nin = len(off)
+
+    Q = {"v": g.vector, "a": g.scalar, "p": g.tensor, "g": g, "y": g.sync}
+    SEM = {"v": "cv", "a": "ca", "p": "cp", "g": "cg"}
+    cnt = {"v": 0, "a": 0, "p": 0, "g": 0}
+    known = {e: {} for e in Q}
+    lastw, readers = {}, {}
+
+    def need(e, tok):
+        sem, n, _src, seen = tok
+        if known[e].get(sem, 0) < n:
+            Q[e].wait_ge(T.sem[sem], n)
+            known[e][sem] = n
+        for s, m in seen.items():
+            if known[e].get(s, 0) < m:
+                known[e][s] = m
+
+    def deps(e, R, W):
+        toks = [lastw[x] for x in R if x in lastw]
+        for x in W:
+            toks += [t for t in readers.get(x, []) + ([lastw[x]] if x in lastw else []) if t[2] != e]
+        toks.sort(key=lambda t: -t[1])
+        for t in toks:
+            need(e, t)
+
+    def op(e, R, W, fn):
+        deps(e, R, W)
+        ins = fn()
+        cnt[e] += 1
+        ins.then_inc(T.sem[SEM[e]], 1)
+        tok = (SEM[e], cnt[e], e, dict(known[e]))
+        for x in R:
+            readers.setdefault(x, []).append(tok)
+        for x in W:
+            lastw[x] = tok
+            readers[x] = []
+
+    def ext(x, sem, n):
+        lastw[x] = (sem, n, None, {})
+
+    V, ACT, PE = g.vector, g.scalar, g.tensor
+
+    def ts(R, W, out, in0, s1, op0, s2=None, op1=None):
+        if op1 is None:
+            op("v", R, W, lambda: V.tensor_scalar(out, in0, s1, None, op0))
+        else:
+            op("v", R, W, lambda: V.tensor_scalar(out, in0, s1, s2, op0, op1))
+
+    def tt(R, W, out, in0, in1, o):
+        op("v", R, W, lambda: V.tensor_tensor(out, in0, in1, o))
+
+    def cp(R, W, out, in_):
+        op("v", R, W, lambda: V.tensor_copy(out, in_))
+
+    def act(R, W, out, in_, bias=0.0, scale=1.0):
+        f = AF.Copy if bias == 0.0 else AF.Identity
+        op("a", R, W, lambda: ACT.activation(out, in_, f, bias=float(bias), scale=float(scale)))
+
+    def tolist(R, bank, x, n, z):
+        def run():
+            for i in range(16):
+                ins = PE.matmul(T[bank][:, 0:n // 16], T[z][:, 15 - i:143 - i], T[x][:, i:n:16], i == 0, i == 15)
+            return ins
+        op("p", R + [x, z], [bank], run)
+
+    def widen(kind, q):
+        w = WB if kind == "B3" else 512
+        op("p", [kind + str(q), "ih"], ["pt%d" % q],
+           lambda: PE.matmul(T["pt%d" % q][:, :], T.ih[:, :], T["s" + kind][:, w * q:w * q + 512], True, True))
+
+    nsent = [0]
+
+    def send(kind, R, to_helpers):
+        deps("g", R, [])
+        src = slot(T, kind, r)
+        if to_helpers:
+            j = 0 if kind in CARRIES[0] else 1
+            trs = []
+            for (able, _q), engs in zip(pairs, (on, off)):
+                rid, pid = topo.addr(able[j], core)
+                trs.append(RemoteDMATransfer(dst_ids=[DstId(rid=rid, pnc=pid)], dma_engine_mask=bits(engs),
+                                             remote_sem=asem(T, kind, r), src=src, dst=src))
+            g.remote_dma_fused(trs, local_sem=T.sem.snd)
+            nsent[0] += len(on) + len(off)
+        else:
+            rid, pid = topo.addr(T.cores[direct], core)
+            g.remote_dma(src, src, asem(T, kind, r), T.sem.snd, pid, rid, bits(off))
+            nsent[0] += len(off)
+
+    nout = [0]
+
+    def store(R, out, in_):
+        deps("y", R, [])
+        g.sync.dma_start(out, in_).then_inc(T.sem.out, 16)
+        nout[0] += 16
+
+    g.sync.dma_start(T.t12[:, 4:72], T.tri[:, 0:68]).then_inc(T.sem.l12, 16)
+    for h in range(2):
+        g.scalar.dma_start(T.lt[:, h], T.let[h::2, 64:1600]).then_inc(T.sem.llt, 16)
+    g.sync.dma_start(T.pr[:, :], T.par[:, :]).then_inc(T.sem.lpr, 16)
+    g.sync.dma_start(T.t3[:, :], T.tri[:, 68:580]).then_inc(T.sem.lt3, 16)
+    for t in range(6):
+        g.scalar.dma_start(T.tx[:, 64 * t:64 * t + 64], T.txt[:, 1024 * t:1024 * t + 1024]).then_inc(T.sem.ltx, 16)
+    g.sync.dma_start(T.t4[:, :], T.tri[:, 580:1092]).then_inc(T.sem.lt4, 16)
+    ext("t12", "l12", 16); ext("lt", "llt", 32); ext("pr", "lpr", 16)
+    ext("t3", "lt3", 16); ext("tx", "ltx", 96); ext("t4", "lt4", 16)
+    ext("Sall", "aS", 3 * nin)
+    for q in order[1:]:
+        for kind in ("B3", "B4", "F"):
+            ext(kind + str(q), "a%s%d" % (kind, q), nin)
+        ext("L%d" % q, "aB3%d" % q, nin)
+
+    op("g", [], ["dm"], lambda: g.iota(T.dm[:, :], [[1, 128]], 0, -1))
+    op("g", [], ["cst"], lambda: g.iota(T.cst[:, :], [[0, 4], [1, 16]], 0, 0, allow_small_or_imprecise_dtypes=True))
+    op("g", [], ["p4"], lambda: g.iota(T.p4[:, :], [[0, 4]], 0, 1))
+    for z in ("zb", "zh", "zf"):
+        if z == "zh":
+            cp(["zb0"], ["zh0"], T.zh[:, :], T.zb[:, :])
+        else:
+            op("v", [], [z + "0"], lambda: V.memset(T[z][:, :], 0.0))
+    op("v", [], ["of1"], lambda: V.memset(T.of12[:, 0:4], 0.0))
+    ts(["dm"], ["sh8"], T.sh8[:, :], T.dm[:, 15:128:16], 4, A.arith_shift_right)
+    ts(["dm"], ["t16"], T.t16[:, :], T.dm[:, 0:16], 15, A.bitwise_and)
+    ts(["p4"], ["ca"], T.ca[:, :], T.p4[:, :], 15, A.bitwise_and)
+    for z in ("zb", "zh", "zf"):
+        ts(["sh8", z + "0", "zh0"], [z], T[z][:, 15:143:16], T.sh8[:, :], 0.0, A.is_equal)
+    ts(["t16"], ["i16"], T.i16[:, :], T.t16[:, :], 0.0, A.is_equal)
+    ts(["dm"], ["ih"], T.ih[:, :], T.dm[:, :], 0.0, A.is_equal)
+    cp(["ca"], ["cl"], T.cl[:, :], T.ca[:, :])
+
+    b2 = 32 + 64 * r
+    ts(["t12"], ["l1"], T.l1[:, :], T.t12[:, 4:8], float(b2), A.subtract)
+    ts(["t12"], ["S1"], T.sS[:, r, 0:4], T.t12[:, 4:8], float(S2), A.subtract)
+    ts(["t12", "l1"], ["S2"], T.sS[:, r, 4:WS], T.t12[:, 8:72].indirect(T.l1[:, :]), float(S2), A.subtract)
+    send("S", ["S1", "S2"], True)
+    send("S", ["S1", "S2"], False)
+
+    for h in range(2):
+        cp(["lt"], ["lt2%d" % h], T.lt2[:, :, 16 * h:16 * h + 16], T.lt[:, h])
+    cp(["cst", "l1"], ["vp"], T.x3[:, 512:576].indirect(T.l1[:, :]), T.cst[:, :])
+    for u in range(3):
+        op("v", ["lt20", "lt21"], ["lt3%d" % u], lambda: V.transpose(T.lt3[:, 32 * u:32 * u + 32], T.lt2[:, u, :]))
+    cp(["pr"], ["pru"], T.pru[:, :], T.pr[:, :])
+    for u in range(3):
+        cp(["lt3%d" % u], ["ltu%d" % u], T.ltu[:, u:96:3], T.lt3[:, 32 * u:32 * u + 32])
+    LT = ["ltu0", "ltu1", "ltu2"]
+    act(LT + ["cst"], ["lb3"], T.lb3[:, :], T.cst[:, 0:16].indirect(T.ltu[:, 0:32]), scale=1.0 / 16)
+    act(LT + ["i16"], ["m4"], T.m4[:, :], T.i16[:, :].indirect(T.ltu[:, 32:64]))
+    o3 = WB * r
+    ts(["pr"], ["a16"], T.a16[:, :], T.pr[:, 0:4], 256.0, A.mult, 1024.0 * r, A.add)
+    ts(["t3"], ["B3%d" % r], T.sB3[:, o3:o3 + 512], T.t3[:, :], float(SH), A.subtract)
+    tt(["vp", "pru", "lb3"], ["x3"], T.x3[:, 0:512], T.x3[:, 512:576].indirect(T.pru[:, 4:36]), T.lb3[:, :], A.add)
+    tolist(["vp"], "pl0", "x3", 576, "zb")
+    act(["x3", "pru"], ["x4i"], T.x4i[:, :], T.x3[:, 0:512].indirect(T.pru[:, 36:68]))
+    ts(["pl0"], ["La"], T.sB3[:, o3 + 512:o3 + 544], T.pl0[:, 0:32], 16.0, A.mult)
+    tt(["pl0", "a16"], ["Lb"], T.sB3[:, o3 + 544:o3 + 548], T.pl0[:, 32:36], T.a16[:, :], A.add)
+    send("B3", ["B3%d" % r, "La", "Lb"], True)
+    send("B3", [], False)
+    tolist([], "pl1", "x4i", 512, "zb")
+    widen("B3", r)
+
+    def mask(t):
+        o = 64 * (t - 2)
+        act(["txu", "i16"], ["mt%d" % t], T.mt[:, 16 * o:16 * o + 1024], T.i16[:, :].indirect(T.txu[:, o:o + 64]))
+
+    def lists(q):
+        R = ["La", "Lb"] if q == r else ["L%d" % q]
+        ts(R, ["lst%d" % q], T.lst[:, 36 * q:36 * q + 36], T.sB3[:, WB * q + 512:WB * q + NB], 1.0 / 16, A.mult)
+
+    cp(["tx"], ["txu"], T.txu[:, :], T.tx[:, 128:384])
+    ts(["tx"], ["ta"], T.ta[:, :], T.tx[:, 0:64], 16.0, A.mult)
+    act(["vp"], ["of2"], T.of12[:, 4:68], T.x3[:, 512:576], bias=16.0)
+    act(["S1"], ["yg1"], T.oyg[:, 0:4], T.sS[:, r, 0:4], bias=S2)
+    mask(2)
+    mask(4)
+    ts(["t4"], ["B4%d" % r], T.sB4[:, 512 * r:512 * r + 512], T.t4[:, :], float(SH), A.subtract)
+    send("B4", ["B4%d" % r], True)
+    send("B4", [], False)
+    op("g", [], ["io"], lambda: g.iota(T["io"][:, :], [[1, 256]], 0, 0, allow_small_or_imprecise_dtypes=True))
+    tt(["ta", "tx"], ["tb"], T.tb[:, :], T.ta[:, :], T.tx[:, 64:128], A.add)
+    lists(r)
+    cp(["pl1"], ["i4"], T.i4[:, :], T.pl1[:, 0:32])
+    cp(["tb"], ["i01"], T.i01[:, :], T.tb[:, :])
+    cp(["txu", "i16"], ["mt3v"], T.mt[:, 1024:2048], T.i16[:, :].indirect(T.txu[:, 64:128]))
+    store(["of1", "of2"], T.yf[:, 0:68], T.of12[0:128:16, :])
+
+    cp(["Sall", "S1"], ["g1"], T.g1[:, :], T.sS[:, :, 0:4])
+    for q in range(4):
+        tt(["g1", "S2", "cl"], ["w2%d" % q], T.w2[:, 64 * q:64 * q + 64], T.g1[:, :].indirect(T.cl[:, :]),
+           T.sS[:, q, 4:WS], A.max)
+    W2 = ["w20", "w21", "w22", "w23"]
+
+    def d3(q):
+        act(W2 + ["lst%d" % q], ["g3%d" % q], T.wg[:, G3 + 512 * q:G3 + 512 * q + 512],
+            T.w2[:, :].indirect(T.lst[:, 36 * q:36 * q + 32]), bias=S2 - SH)
+
+    def g2(q):
+        act(W2 + ["lst%d" % q], ["g2%d" % q], T.wg[:, 64 * q:64 * q + 64],
+            T.w2[:, :].indirect(T.lst[:, 36 * q + 32:36 * q + 36]), bias=S2 - SH)
+
+    def top(name, o, q):
+        a = T.wg[:, o + 512 * q:o + 512 * q + 512]
+        tt([name + str(q), "pt%d" % q], [name + str(q)], a, a, T["pt%d" % q][:, :], A.max)
+
+    G23 = ["g2%d" % q for q in range(4)] + ["g3%d" % q for q in range(4)]
+    GG = G23 + ["g4%d" % q for q in range(4)]
+    w23, wgg = T.wg[:, 0:G4], T.wg[:, 0:GE]
+
+    tt(W2 + ["i4", "m4"], ["xf4"], T.xf4[:, :], T.w2[:, :].indirect(T.i4[:, :]), T.m4[:, :], A.mult)
+    d3(r); g2(r)
+    tolist([], "pl2", "xf4", 512, "zh")
+    lists(direct)
+    ts(["g1"], ["l1a"], T.l1a[:, :], T.g1[:, :], float(S2 - 32), A.add)
+    d3(direct); g2(direct)
+    act(["io", "l1a"], ["n2"], T.n2[:, :], T["io"][:, :].indirect(T.l1a[:, :]), scale=1.0 / 16)
+    tt(W2 + ["i01", "mt2"], ["xh0"], T.xh[:, 0:512], T.w2[:, :].indirect(T.i01[:, 0:32]), T.mt[:, 0:512], A.mult)
+    ts(["pl2"], ["F%d" % r], slot(T, "F", r), T.pl2[:, 0:32], float(S2 - 32), A.add)
+    send("F", ["F%d" % r], True)
+    send("F", [], False)
+    widen("B3", direct)
+    tt(W2 + ["i01", "mt2"], ["xh"], T.xh[:, 512:1024], T.w2[:, :].indirect(T.i01[:, 32:64]), T.mt[:, 512:1024], A.mult)
+    tolist(["xh0"], "pl3", "xh", 1024, "zh")
+    lists(c1); lists(c2)
+    widen("B3", c1); widen("B3", c2)
+    d3(c1); d3(c2); g2(c1); g2(c2)
+    top("g3", G3, r); top("g3", G3, direct)
+    ts(["pl3"], ["i3"], T.i3[:, :], T.pl3[:, 0:64], float(S2 - 32), A.add)
+    ts(["pl3"], ["mx"], T.mx[:, :], T.pl3[:, 0:64], float(S2 - SH), A.add)
+    ts(["pl2"], ["fl4"], T.fl[:, 0:32], T.pl2[:, 0:32], float(S2), A.add)
+    top("g3", G3, c1); top("g3", G3, c2)
+    widen("B4", r); widen("B4", direct)
+
+    tt(G23 + ["i3", "mt3v"], ["xa"], T.xa[:, :], w23.indirect(T.i3[:, :]), T.mt[:, 1024:2048], A.mult)
+    for q in order:
+        act(G23 + ["F%d" % q], ["g4%d" % q], T.wg[:, G4 + 512 * q:G4 + 512 * q + 512], w23.indirect(slot(T, "F", q)))
+    act(["n2", "i01"], ["xs"], T.xs[:, :], T.n2[:, :].indirect(T.i01[:, :]))
+    mask(5)
+    tolist([], "pl0", "xa", 1024, "zf")
+    cp(LT + ["i16"], ["m5"], T.m5[:, :], T.i16[:, :].indirect(T.ltu[:, 64:96]))
+    tt(["g4%d" % r, "pru", "m5"], ["xb"], T.xb[:, :],
+       T.wg[:, G4 + 512 * r:G4 + 512 * r + 512].indirect(T.pru[:, 68:100]), T.m5[:, :], A.mult)
+    widen("B4", c1); widen("B4", c2)
+    ts(["pl0"], ["i4g"], T.i4g[:, :], T.pl0[:, 0:64], float(SH - 32), A.add)
+    tt(["pl0", "mx"], ["mx"], T.mx[:, :], T.pl0[:, 0:64], T.mx[:, :], A.max)
+    tolist([], "pl3", "xs", 1024, "zb")
+
+    tt(GG + ["i4g", "mt4"], ["xc"], T.xc[:, :], wgg.indirect(T.i4g[:, :]), T.mt[:, 2048:3072], A.mult)
+    act(["g2%d" % r], ["yg2"], T.oyg[:, 4:68], T.wg[:, 64 * r:64 * r + 64], bias=SH)
+    act(["g3%d" % r], ["yg3"], T.oyg[:, 68:580], T.wg[:, G3 + 512 * r:G3 + 512 * r + 512], bias=SH)
+    store(["yg1", "yg2", "yg3"], T.yg[:, 0:580], T.oyg[:, 0:580])
+    tolist([], "pl2", "xc", 1024, "zf")
+    tolist([], "pl1", "xb", 512, "zf")
+    deps("v", ["xc"], [])
+    for q in order:
+        top("g4", G4, q)
+    act(["g4%d" % r], ["yg4"], T.oyg[:, 580:1092], T.wg[:, G4 + 512 * r:G4 + 512 * r + 512], bias=SH)
+    store(["yg4"], T.yg[:, 580:1092], T.oyg[:, 580:1092])
+    act(["n2", "lst%d" % r], ["of3"], T.of3[:, :], T.n2[:, :].indirect(T.lst[:, 36 * r:36 * r + 32]), bias=32.0, scale=16.0)
+    store(["of3"], T.yf[:, 68:580], T.of3[0:128:16, :])
+    ts(["pl2"], ["i5"], T.i5[:, :], T.pl2[:, 0:64], float(SH - 32), A.add)
+    tt(["pl2", "mx"], ["mx"], T.mx[:, :], T.pl2[:, 0:64], T.mx[:, :], A.max)
+
+    tt(GG + ["i5", "mt5"], ["xa"], T.xa[:, :], wgg.indirect(T.i5[:, :]), T.mt[:, 3072:4096], A.mult)
+    tolist([], "pl0", "xa", 1024, "zf")
+    ts(["pl3"], ["uc"], T.uc[:, :], T.pl3[:, 0:64], 32.0, A.add)
+    ts(["mx"], ["mx"], T.mx[:, :], T.mx[:, :], float(SH), A.add)
+    ts(["pl1"], ["if5"], T.if5[:, :], T.pl1[:, 0:32], float(SH - 32), A.add)
+    ts(["pl1"], ["fl5"], T.fl[:, 32:64], T.pl1[:, 0:32], float(SH), A.add)
+    act(GG + ["if5"], ["yg5"], T.oyg[:, 1092:1604], wgg.indirect(T.if5[:, :]), bias=SH)
+    op("v", ["fl4", "fl5"], ["ft"], lambda: V.transpose(T.ft[:, :], T.fl[:, :]))
+    for l in range(2):
+        for h in range(2):
+            store(["ft"], T.yf[h::2, 580 + 512 * l:1092 + 512 * l], T.ft[:, 32 * l + 16 * h:32 * l + 16 * h + 16])
+    store(["yg5"], T.yg[:, 1092:1604], T.oyg[:, 1092:1604])
+    tt(GG + ["i4g", "mt4"], ["xh", "xh0"], T.xh[:, :], wgg.indirect(T.i4g[:, :]), T.mt[:, 2048:3072], A.mult)
+    tolist([], "pl2", "xh", 1024, "zh")
+    tt(["uc", "mx"], ["mx"], T.mx[:, :], T.uc[:, :], T.mx[:, :], A.max)
+    ts(["pl0"], ["oyl"], T.oyl[:, :], T.pl0[:, 0:64], float(SH), A.add)
+    store(["oyl"], T.yl[:, :], T.oyl[:, :])
+    tt(["oyl", "mx"], ["mx"], T.mx[:, :], T.oyl[:, :], T.mx[:, :], A.max)
+    ts(["pl2"], ["va"], T.va[:, :], T.pl2[:, 0:64], 0.0, A.is_ge, float(SH), A.mult)
+    tt(["pl2", "va"], ["vb"], T.vb[:, :], T.pl2[:, 0:64], T.va[:, :], A.add)
+    tt(["vb", "mx"], ["oym"], T.oym[:, :], T.vb[:, :], T.mx[:, :], A.max)
+    store(["oym"], T.ym[:, :], T.oym[:, :])
+
+    g.wait_ge(T.sem.snd, nsent[0])
+    for e in ("v", "a", "p", "g"):
+        need("y", (SEM[e], cnt[e], e, {}))
+    g.sync.wait_ge(T.sem.out, nout[0])

@@ -1,69 +1,52 @@
 from concourse.bass import DstId, RemoteDMATransfer
 from concourse.mybir import AluOpType as A, ActivationFunctionType as AF
 
-SH = 4384
 S2 = 1184
-WS, WB, NB, WF = 68, 552, 548, 32
+C0 = 2592
+WS, WB, NB, WF, PAD = 68, 552, 548, 32, 16
 G3, G4, GE = 256, 2304, 4352
+K5 = 256
+LIFT = 288
 
-SCRATCH = {
-    "t12": ("sbuf", [128, 72], "int32"), "t3": ("sbuf", [128, 512], "int32"), "t4": ("sbuf", [128, 512], "int32"),
-    "pr": ("sbuf", [128, 100], "int32"), "pru": ("sbuf", [128, 100], "uint16"),
-    "lt": ("sbuf", [128, 2, 3, 16], "int32"), "lt2": ("sbuf", [128, 3, 32], "int32"),
-    "lt3": ("sbuf", [128, 96], "int32"), "ltu": ("sbuf", [128, 96], "uint16"),
-    "tx": ("sbuf", [128, 384], "int32"), "txu": ("sbuf", [128, 256], "uint16"),
-    "ta": ("sbuf", [128, 64], "float32"), "tb": ("sbuf", [128, 64], "float32"), "i01": ("sbuf", [128, 64], "uint16"),
-    "cst": ("sbuf", [128, 64], "bfloat16"), "dm": ("sbuf", [128, 128], "int32"), "p4": ("sbuf", [128, 4], "int32"),
-    "io": ("sbuf", [128, 256], "bfloat16"),
-    "sh8": ("sbuf", [128, 8], "int32"), "t16": ("sbuf", [128, 16], "int32"), "i16": ("sbuf", [128, 16], "bfloat16"),
-    "zb": ("sbuf", [128, 144], "bfloat16"), "zh": ("sbuf", [128, 144], "float16"), "zf": ("sbuf", [128, 144], "float32"),
-    "ih": ("sbuf", [128, 128], "float16"),
-    "ca": ("sbuf", [128, 4], "int32"), "cl": ("sbuf", [128, 4], "uint16"), "g1": ("sbuf", [128, 16], "float32"),
-    "l1": ("sbuf", [128, 4], "uint16"), "l1a": ("sbuf", [128, 16], "uint16"), "a16": ("sbuf", [128, 4], "float32"),
-    "lb3": ("sbuf", [128, 512], "bfloat16"), "x3": ("sbuf", [128, 576], "bfloat16"), "x4i": ("sbuf", [128, 512], "bfloat16"),
-    "i4": ("sbuf", [128, 32], "uint16"),
-    "m4": ("sbuf", [128, 512], "bfloat16"), "m5": ("sbuf", [128, 512], "bfloat16"), "mt": ("sbuf", [128, 4096], "bfloat16"),
-    "sS": ("sbuf", [128, 4, WS], "float32"), "sB3": ("sbuf", [128, 4 * WB], "float16"),
-    "sB4": ("sbuf", [128, 2048], "float16"), "sF": ("sbuf", [128, 4 * WF], "uint16"),
-    "lst": ("sbuf", [128, 144], "uint16"),
-    "w2": ("sbuf", [128, 256], "float32"), "wg": ("sbuf", [128, GE], "float32"), "n2": ("sbuf", [128, 256], "bfloat16"),
-    "xf4": ("sbuf", [128, 512], "float16"), "xh": ("sbuf", [128, 1024], "float16"), "xa": ("sbuf", [128, 1024], "float32"),
-    "xb": ("sbuf", [128, 512], "float32"), "xc": ("sbuf", [128, 1024], "float32"), "xs": ("sbuf", [128, 1024], "bfloat16"),
-    "i3": ("sbuf", [128, 64], "uint16"), "i4g": ("sbuf", [128, 64], "uint16"),
-    "i5": ("sbuf", [128, 64], "uint16"), "if5": ("sbuf", [128, 32], "uint16"),
-    "uc": ("sbuf", [128, 64], "float32"), "va": ("sbuf", [128, 64], "float32"), "vb": ("sbuf", [128, 64], "float32"),
-    "mx": ("sbuf", [128, 64], "float32"), "oyl": ("sbuf", [128, 64], "float32"), "oym": ("sbuf", [128, 64], "float32"),
-    "fl": ("sbuf", [128, 64], "float32"), "ft": ("sbuf", [128, 64], "float32"),
-    "oyg": ("sbuf", [128, 1604], "float32"), "of12": ("sbuf", [128, 68], "float32"), "of3": ("sbuf", [128, 512], "float32"),
-    "pt0": ("psum", [128, 512], "float32"), "pt1": ("psum", [128, 512], "float32"),
-    "pt2": ("psum", [128, 512], "float32"), "pt3": ("psum", [128, 512], "float32"),
-    "pl0": ("psum", [128, 512], "float32"), "pl1": ("psum", [128, 512], "float32"),
-    "pl2": ("psum", [128, 512], "float32"), "pl3": ("psum", [128, 512], "float32"),
+F32, BF, F16, I32, U16 = "float32", "bfloat16", "float16", "int32", "uint16"
+SB = {
+    I32: dict(t12=72, t3=512, t4=512, pr=100, lb=576, lt3=64, tx=384, dm=144, p4=4, sh8=8, t16=16, ca=4, r0=64),
+    U16: dict(pru=100, ltu=64, txu=256, i01=64, cl=4, l1=4, l1a=16, i4=32, sF=4 * WF, lst=144,
+              i3=64, i4g=64, ip=64, i5=64, if5=32),
+    BF: dict(nat=256, i16=16, zb=144, iw=144, crow=1024, ones=512, l2w=64, x3=576, x4i=512, m4=512, m5=512, mt=4096,
+             sB3=4 * WB, sB4=PAD + 2048, n2=256, xp=1024, crt=64),
+    F16: dict(zh=144, xf4=512, xh=1024, xs=1024, xy=1024),
+    F32: dict(zf=144, z2=136, sw=512, lo=1, hi=1, g1=16, a16=4, ta=64, tb=64, tf=128, w2=256, wg=GE,
+              xa=1024, xb=512, xc=1024, a3=64, mp=64, mx=64, va=64, vb=64, oyl=64, oym=64, fa=32, fb=32, fl=64, ft=64,
+              o1=4, o5=512, of12=68, of3=512),
 }
-SEMAPHORES = (["cv", "ca", "cp", "cg", "l12", "lpr", "llt", "lt3", "lt4", "ltx", "out", "snd", "aS"]
+SCRATCH = {n: ("sbuf", [128, w], d) for d, b in SB.items() for n, w in b.items()}
+SCRATCH.update(lt=("sbuf", [128, 2, 2, 16], I32), lt2=("sbuf", [128, 2, 32], I32), sS=("sbuf", [128, 4, WS + 4], F16))
+BANKS = ["pt0", "pt1", "pt2", "pt3", "pa0", "pa1", "pl0", "pl1"]
+SCRATCH.update({b: ("psum", [128, 512], F32) for b in BANKS})
+SEMAPHORES = (["cv", "ca", "cp", "cg", "l12", "lpr", "llb", "llt", "lt3", "lt4", "lx0", "lx2", "lx3", "lx4", "out", "snd", "aS"]
               + ["a%s%d" % (k, q) for k in ("B3", "B4", "F") for q in range(4)])
-CARRIES = (("S", "B3", "F"), ("B4",))
 
 
 def routes(T, topo, rank):
     core = T.cores[rank]
     others = [q for q in range(len(T.cores)) if q != rank]
-    direct = [q for q in others if topo.may_write(core, T.cores[q])]
-    cross = [q for q in others if q not in direct]
-    cross.sort(key=lambda q: topo.host(T.cores[q]) != topo.host(core))
-    pairs = []
-    for k, q in enumerate(cross):
-        able = [h for h in topo.cores_of(core) if h != core and topo.may_write(h, T.cores[q])
-                and (topo.die(h) == topo.die(core)) == (k == 0)]
-        pairs.append((able, q))
-    return direct[0], pairs
+    direct = [q for q in others if topo.may_write(core, T.cores[q])][0]
+    cross = sorted((q for q in others if q != direct), key=lambda q: topo.host(T.cores[q]) != topo.host(core))
+    able = [h for h in topo.cores_of(core) if h != core and topo.may_write(h, T.cores[cross[0]])]
+    near = [h for h in able if topo.die(h) == topo.die(core)]
+    far = [h for h in able if h not in near]
+    off = topo.engines(core, T.cores[direct])
+    on = [e for e in topo.engines(core, near[0]) if e not in off]
+    return direct, cross, [(near[0], on, ("S", "B3", "F"), cross[:1]), (far[0], off, ("S", "B3", "F"), cross[1:]),
+                           (far[1], on, ("B4",), cross)]
 
 
 def slot(T, kind, q):
     if kind == "S":
-        return T.sS[:, q, :]
-    w, n = {"B3": (WB, NB), "B4": (512, 512), "F": (WF, WF)}[kind]
-    return T["s" + kind][:, w * q:w * q + n]
+        return T.sS[:, q, 0:WS]
+    o, w, n = {"B3": (0, WB, NB), "B4": (PAD, 512, 512), "F": (0, WF, WF)}[kind]
+    return T["s" + kind][:, o + w * q:o + w * q + n]
 
 
 def asem(T, kind, q):
@@ -74,24 +57,15 @@ def bits(engs):
     return sum(1 << e for e in engs)
 
 
-def split(topo, core, T, rank):
-    d, pairs = routes(T, topo, rank)
-    off = topo.engines(core, T.cores[d])
-    on = [e for e in topo.engines(core, pairs[0][0][0]) if e not in off]
-    return on, off
-
-
-def helper_program(g, core, T, topo, rank, k, kinds):
-    d, pairs = routes(T, topo, rank)
-    n_in = len(split(topo, T.cores[rank], T, rank)[k])
-    dst = T.cores[pairs[k][1]]
-    rid, pid = topo.addr(dst, core)
+def helper_program(g, core, T, topo, rank, engs, kinds, ranks):
     sent = 0
     for kind in kinds:
-        g.wait_ge(asem(T, kind, rank), n_in)
-        g.remote_dma(slot(T, kind, rank), slot(T, kind, rank), asem(T, kind, rank), T.sem.snd, pid, rid,
-                     topo.mask(core, dst))
-        sent += len(topo.engines(core, dst))
+        g.wait_ge(asem(T, kind, rank), len(engs))
+        for q in ranks:
+            rid, pid = topo.addr(T.cores[q], core)
+            g.remote_dma(slot(T, kind, rank), slot(T, kind, rank), asem(T, kind, rank), T.sem.snd, pid, rid,
+                         topo.mask(core, T.cores[q]))
+            sent += len(topo.engines(core, T.cores[q]))
     g.wait_ge(T.sem.snd, sent)
 
 
@@ -99,15 +73,13 @@ def rank_program(g, core, T, topo):
     r = T.rank_of(core)
     if r is None:
         for q in range(len(T.cores)):
-            for k, (able, _d) in enumerate(routes(T, topo, q)[1]):
-                for j, kinds in enumerate(CARRIES):
-                    if able[j] == core:
-                        helper_program(g, core, T, topo, q, k, kinds)
+            for h, engs, kinds, ranks in routes(T, topo, q)[2]:
+                if h == core:
+                    helper_program(g, core, T, topo, q, engs, kinds, ranks)
         return
 
-    direct, pairs = routes(T, topo, r)
-    on, off = split(topo, core, T, r)
-    c1, c2 = pairs[0][1], pairs[1][1]
+    direct, (c1, c2), helpers = routes(T, topo, r)
+    off = topo.engines(core, T.cores[direct])
     order = [r, direct, c1, c2]
     nin = len(off)
 
@@ -115,7 +87,7 @@ def rank_program(g, core, T, topo):
     SEM = {"v": "cv", "a": "ca", "p": "cp", "g": "cg"}
     cnt = {"v": 0, "a": 0, "p": 0, "g": 0}
     known = {e: {} for e in Q}
-    lastw, readers = {}, {}
+    lastw, readers, bank = {}, {}, {}
 
     def need(e, tok):
         sem, n, _src, seen = tok
@@ -130,6 +102,7 @@ def rank_program(g, core, T, topo):
         toks = [lastw[x] for x in R if x in lastw]
         for x in W:
             toks += [t for t in readers.get(x, []) + ([lastw[x]] if x in lastw else []) if t[2] != e]
+        toks += [bank[x] for x in R + W if x in bank and bank[x][2] != e]
         toks.sort(key=lambda t: -t[1])
         for t in toks:
             need(e, t)
@@ -145,11 +118,15 @@ def rank_program(g, core, T, topo):
         for x in W:
             lastw[x] = tok
             readers[x] = []
+        for x in R + W:
+            if x in BANKS:
+                bank[x] = tok
 
     def ext(x, sem, n):
         lastw[x] = (sem, n, None, {})
 
     V, ACT, PE = g.vector, g.scalar, g.tensor
+    IB = T.iw[:, 8:136]
 
     def ts(R, W, out, in0, s1, op0, s2=None, op1=None):
         if op1 is None:
@@ -163,137 +140,195 @@ def rank_program(g, core, T, topo):
     def cp(R, W, out, in_):
         op("v", R, W, lambda: V.tensor_copy(out, in_))
 
-    def act(R, W, out, in_, bias=0.0, scale=1.0):
-        f = AF.Copy if bias == 0.0 else AF.Identity
-        op("a", R, W, lambda: ACT.activation(out, in_, f, bias=float(bias), scale=float(scale)))
+    def fill(W, out, c):
+        op("v", [], W, lambda: V.memset(out, c))
 
-    def tolist(R, bank, x, n, z):
+    def act(R, W, out, in_, bias=0.0, scale=1.0, f=None):
+        f = f or (AF.Copy if bias == 0.0 else AF.Identity)
+        op("a", R, W, lambda: ACT.activation(out, in_, f, bias=float(bias), scale=scale))
+
+    def count(W, out, pattern, start, step):
+        op("g", [], W, lambda: g.iota(out, pattern, start, step, allow_small_or_imprecise_dtypes=True))
+
+    def mms(R, W, calls):
         def run():
-            for i in range(16):
-                ins = PE.matmul(T[bank][:, 0:n // 16], T[z][:, 15 - i:143 - i], T[x][:, i:n:16], i == 0, i == 15)
+            for c in calls:
+                ins = PE.matmul(*c)
             return ins
-        op("p", R + [x, z], [bank], run)
+        op("p", R, W, run)
+
+    def tolist(R, b, x, n, z, rows=range(16)):
+        mms(R + [z], [b], [(T[b][:, 0:n // 16], T[z][:, 15 - i:143 - i], T[x][:, i:n:16], i == 0, i == 15)
+                           for i in rows])
+
+    def halflist(R, b, x, h, z, last=True):
+        mms(R + [z], [b], [(T[b][:, 0:64], T[z][:, 15 - 8 * h - i:143 - 8 * h - i], T[x][:, 512 * h + i:512 * h + 512:8],
+                            h == 0 and i == 0, last and h == 1 and i == 7) for i in range(8)])
+
+    def swap(R, b, x, o):
+        mms(R + ["sw"], [b], [(T[b][:, o + 32 * u:o + 32 * u + 32], T.sw[:, 128 * (2 * u + h):128 * (2 * u + h) + 128],
+                               T[x][:, o + 32 * h:o + 32 * h + 32], h == 0, h == 1) for u in range(2) for h in range(2)])
+
+    def bases(l):
+        count(["crow%d" % l], T.crow[0:1, 512 * l:512 * l + 512], [[512, 4], [0, 128]], C0 + 2048 * l, 0)
+
+    def base(l, q):
+        k = 4 * l + q
+        mms(["crow%d" % l, "ones"], ["pt%d" % q],
+            [(T["pt%d" % q][:, :], T.crow[0:1, 128 * k:128 * k + 128], T.ones[0:1, :], True, False)])
 
     def widen(kind, q):
-        w = WB if kind == "B3" else 512
-        op("p", [kind + str(q), "ih"], ["pt%d" % q],
-           lambda: PE.matmul(T["pt%d" % q][:, :], T.ih[:, :], T["s" + kind][:, w * q:w * q + 512], True, True))
+        mms([kind + str(q), "ib"], ["pt%d" % q],
+            [(T["pt%d" % q][:, :], IB, slot(T, kind, q) if kind == "B4" else T.sB3[:, WB * q:WB * q + 512], False, True)])
 
     nsent = [0]
 
-    def send(kind, R, to_helpers):
+    def hand(kind, R):
         deps("g", R, [])
-        src = slot(T, kind, r)
-        if to_helpers:
-            j = 0 if kind in CARRIES[0] else 1
-            trs = []
-            for (able, _q), engs in zip(pairs, (on, off)):
-                rid, pid = topo.addr(able[j], core)
+        src, trs = slot(T, kind, r), []
+        for h, engs, kinds, _ranks in helpers:
+            if kind in kinds:
+                rid, pid = topo.addr(h, core)
                 trs.append(RemoteDMATransfer(dst_ids=[DstId(rid=rid, pnc=pid)], dma_engine_mask=bits(engs),
                                              remote_sem=asem(T, kind, r), src=src, dst=src))
-            g.remote_dma_fused(trs, local_sem=T.sem.snd)
-            nsent[0] += len(on) + len(off)
-        else:
-            rid, pid = topo.addr(T.cores[direct], core)
-            g.remote_dma(src, src, asem(T, kind, r), T.sem.snd, pid, rid, bits(off))
-            nsent[0] += len(off)
+                nsent[0] += len(engs)
+        g.remote_dma_fused(trs, local_sem=T.sem.snd)
+
+    def straight(kind):
+        rid, pid = topo.addr(T.cores[direct], core)
+        g.remote_dma(slot(T, kind, r), slot(T, kind, r), asem(T, kind, r), T.sem.snd, pid, rid, bits(off))
+        nsent[0] += len(off)
+
+    def send(kind, R):
+        hand(kind, R)
+        straight(kind)
 
     nout = [0]
 
-    def store(R, out, in_):
-        deps("y", R, [])
-        g.sync.dma_start(out, in_).then_inc(T.sem.out, 16)
+    def store(R, out, in_, e="y"):
+        deps(e, R, [])
+        Q[e].dma_start(out, in_).then_inc(T.sem.out, 16)
         nout[0] += 16
 
-    g.sync.dma_start(T.t12[:, 4:72], T.tri[:, 0:68]).then_inc(T.sem.l12, 16)
-    for h in range(2):
-        g.scalar.dma_start(T.lt[:, h], T.let[h::2, 64:1600]).then_inc(T.sem.llt, 16)
-    g.sync.dma_start(T.pr[:, :], T.par[:, :]).then_inc(T.sem.lpr, 16)
-    g.sync.dma_start(T.t3[:, :], T.tri[:, 68:580]).then_inc(T.sem.lt3, 16)
-    for t in range(6):
-        g.scalar.dma_start(T.tx[:, 64 * t:64 * t + 64], T.txt[:, 1024 * t:1024 * t + 1024]).then_inc(T.sem.ltx, 16)
-    g.sync.dma_start(T.t4[:, :], T.tri[:, 580:1092]).then_inc(T.sem.lt4, 16)
-    ext("t12", "l12", 16); ext("lt", "llt", 32); ext("pr", "lpr", 16)
-    ext("t3", "lt3", 16); ext("tx", "ltx", 96); ext("t4", "lt4", 16)
+    def load(e, x, sem, pairs_):
+        for out, in_ in pairs_:
+            Q[e].dma_start(out, in_).then_inc(T.sem[sem], 16)
+        ext(x, sem, 16 * len(pairs_))
+
+    def text(t):
+        return T.tx[:, 64 * t:64 * t + 64], T.txt[:, 1024 * t:1024 * t + 1024]
+
+    fill(["lb0"], T.lb[:, :], 0)
+    load("y", "t12", "l12", [(T.t12[:, 4:72], T.tri[:, 0:68])])
+    load("y", "tx2", "lx2", [text(2)])
+    load("y", "pr", "lpr", [(T.pr[:, :], T.par[:, :])])
+    load("y", "tx3", "lx3", [text(3)])
+    deps("a", ["lb0"], [])
+    load("a", "tx4", "lx4", [text(4), text(5)])
+    load("a", "lt", "llt", [(T.lt[:, h], T.let[h::2, 576:1600]) for h in range(2)])
+    load("a", "tx0", "lx0", [text(0), text(1)])
+    deps("y", ["lb0"], [])
+    load("y", "lb", "llb", [(T.lb[0:128:16, :], T.let[:, 0:576])])
+    load("y", "t3", "lt3", [(T.t3[:, :], T.tri[:, 68:580])])
+    load("y", "t4", "lt4", [(T.t4[:, :], T.tri[:, 580:1092])])
     ext("Sall", "aS", 3 * nin)
     for q in order[1:]:
         for kind in ("B3", "B4", "F"):
             ext(kind + str(q), "a%s%d" % (kind, q), nin)
         ext("L%d" % q, "aB3%d" % q, nin)
 
-    op("g", [], ["dm"], lambda: g.iota(T.dm[:, :], [[1, 128]], 0, -1))
-    op("g", [], ["cst"], lambda: g.iota(T.cst[:, :], [[0, 4], [1, 16]], 0, 0, allow_small_or_imprecise_dtypes=True))
     op("g", [], ["p4"], lambda: g.iota(T.p4[:, :], [[0, 4]], 0, 1))
-    for z in ("zb", "zh", "zf"):
-        if z == "zh":
-            cp(["zb0"], ["zh0"], T.zh[:, :], T.zb[:, :])
-        else:
-            op("v", [], [z + "0"], lambda: V.memset(T[z][:, :], 0.0))
-    op("v", [], ["of1"], lambda: V.memset(T.of12[:, 0:4], 0.0))
-    ts(["dm"], ["sh8"], T.sh8[:, :], T.dm[:, 15:128:16], 4, A.arith_shift_right)
-    ts(["dm"], ["t16"], T.t16[:, :], T.dm[:, 0:16], 15, A.bitwise_and)
+    op("g", [], ["dm"], lambda: g.iota(T.dm[:, :], [[1, 144]], -8, -1))
+    bases(0)
+    fill(["zb0"], T.zb[:, :], 0.0)
     ts(["p4"], ["ca"], T.ca[:, :], T.p4[:, :], 15, A.bitwise_and)
-    for z in ("zb", "zh", "zf"):
-        ts(["sh8", z + "0", "zh0"], [z], T[z][:, 15:143:16], T.sh8[:, :], 0.0, A.is_equal)
+    ts(["dm"], ["ib"], T.iw[:, :], T.dm[:, :], 0.0, A.is_equal)
+    ts(["ca"], ["lo"], T.lo[:, :], T.ca[:, 0:1], 8.0, A.is_lt)
+    ts(["ca"], ["hi"], T.hi[:, :], T.ca[:, 0:1], 8.0, A.is_ge)
+    ts(["dm"], ["sh8"], T.sh8[:, :], T.dm[:, 23:144:16], 4, A.arith_shift_right)
+    ts(["dm"], ["t16"], T.t16[:, :], T.dm[:, 8:24], 15, A.bitwise_and)
+    fill(["z20"], T.z2[:, :], 0.0)
+    ts(["sh8", "zb0"], ["zb"], T.zb[:, 15:143:16], T.sh8[:, :], 0.0, A.is_equal)
     ts(["t16"], ["i16"], T.i16[:, :], T.t16[:, :], 0.0, A.is_equal)
-    ts(["dm"], ["ih"], T.ih[:, :], T.dm[:, :], 0.0, A.is_equal)
+    for o in (7, 15):
+        ts(["sh8", "z20"], ["z2"], T.z2[:, o:o + 120:16], T.sh8[:, :], 0.0, A.is_equal)
     cp(["ca"], ["cl"], T.cl[:, :], T.ca[:, :])
+    for u in range(2):
+        for h in range(2):
+            k, o = 128 * (2 * u + h), 8 - 8 * (h - u)
+            act(["ib", "lo", "hi"], ["sw"], T.sw[:, k:k + 128], T.iw[:, o:o + 128], scale=(T.lo, T.hi)[u][:, :])
+    act(["zb"], ["zh"], T.zh[:, :], T.zb[:, :])
+    act(["zb"], ["zf"], T.zf[:, :], T.zb[:, :])
 
-    b2 = 32 + 64 * r
-    ts(["t12"], ["l1"], T.l1[:, :], T.t12[:, 4:8], float(b2), A.subtract)
+    ts(["t12"], ["l1"], T.l1[:, :], T.t12[:, 4:8], float(32 + 64 * r), A.subtract)
     ts(["t12"], ["S1"], T.sS[:, r, 0:4], T.t12[:, 4:8], float(S2), A.subtract)
     ts(["t12", "l1"], ["S2"], T.sS[:, r, 4:WS], T.t12[:, 8:72].indirect(T.l1[:, :]), float(S2), A.subtract)
-    send("S", ["S1", "S2"], True)
-    send("S", ["S1", "S2"], False)
+    send("S", ["S1", "S2"])
+    fill(["pad"], T.sB4[:, 0:PAD], -32768.0)
 
-    for h in range(2):
-        cp(["lt"], ["lt2%d" % h], T.lt2[:, :, 16 * h:16 * h + 16], T.lt[:, h])
-    cp(["cst", "l1"], ["vp"], T.x3[:, 512:576].indirect(T.l1[:, :]), T.cst[:, :])
-    for u in range(3):
-        op("v", ["lt20", "lt21"], ["lt3%d" % u], lambda: V.transpose(T.lt3[:, 32 * u:32 * u + 32], T.lt2[:, u, :]))
-    cp(["pr"], ["pru"], T.pru[:, :], T.pr[:, :])
-    for u in range(3):
-        cp(["lt3%d" % u], ["ltu%d" % u], T.ltu[:, u:96:3], T.lt3[:, 32 * u:32 * u + 32])
-    LT = ["ltu0", "ltu1", "ltu2"]
-    act(LT + ["cst"], ["lb3"], T.lb3[:, :], T.cst[:, 0:16].indirect(T.ltu[:, 0:32]), scale=1.0 / 16)
-    act(LT + ["i16"], ["m4"], T.m4[:, :], T.i16[:, :].indirect(T.ltu[:, 32:64]))
     o3 = WB * r
-    ts(["pr"], ["a16"], T.a16[:, :], T.pr[:, 0:4], 256.0, A.mult, 1024.0 * r, A.add)
-    ts(["t3"], ["B3%d" % r], T.sB3[:, o3:o3 + 512], T.t3[:, :], float(SH), A.subtract)
-    tt(["vp", "pru", "lb3"], ["x3"], T.x3[:, 0:512], T.x3[:, 512:576].indirect(T.pru[:, 4:36]), T.lb3[:, :], A.add)
-    tolist(["vp"], "pl0", "x3", 576, "zb")
-    act(["x3", "pru"], ["x4i"], T.x4i[:, :], T.x3[:, 0:512].indirect(T.pru[:, 36:68]))
-    ts(["pl0"], ["La"], T.sB3[:, o3 + 512:o3 + 544], T.pl0[:, 0:32], 16.0, A.mult)
-    tt(["pl0", "a16"], ["Lb"], T.sB3[:, o3 + 544:o3 + 548], T.pl0[:, 32:36], T.a16[:, :], A.add)
-    send("B3", ["B3%d" % r, "La", "Lb"], True)
-    send("B3", [], False)
-    tolist([], "pl1", "x4i", 512, "zb")
-    widen("B3", r)
 
-    def mask(t):
+    def mask(t, a=0, b=1024):
         o = 64 * (t - 2)
-        act(["txu", "i16"], ["mt%d" % t], T.mt[:, 16 * o:16 * o + 1024], T.i16[:, :].indirect(T.txu[:, o:o + 64]))
+        return T.mt[:, 16 * o + a:16 * o + b], T.i16[:, :].indirect(T.txu[:, o + a // 16:o + b // 16])
 
     def lists(q):
         R = ["La", "Lb"] if q == r else ["L%d" % q]
-        ts(R, ["lst%d" % q], T.lst[:, 36 * q:36 * q + 36], T.sB3[:, WB * q + 512:WB * q + NB], 1.0 / 16, A.mult)
+        (cp if q == r else act)(R, ["lst%d" % q], T.lst[:, 36 * q:36 * q + 36], T.sB3[:, WB * q + 512:WB * q + NB])
 
-    cp(["tx"], ["txu"], T.txu[:, :], T.tx[:, 128:384])
-    ts(["tx"], ["ta"], T.ta[:, :], T.tx[:, 0:64], 16.0, A.mult)
-    act(["vp"], ["of2"], T.of12[:, 4:68], T.x3[:, 512:576], bias=16.0)
-    act(["S1"], ["yg1"], T.oyg[:, 0:4], T.sS[:, r, 0:4], bias=S2)
-    mask(2)
-    mask(4)
-    ts(["t4"], ["B4%d" % r], T.sB4[:, 512 * r:512 * r + 512], T.t4[:, :], float(SH), A.subtract)
-    send("B4", ["B4%d" % r], True)
-    send("B4", [], False)
-    op("g", [], ["io"], lambda: g.iota(T["io"][:, :], [[1, 256]], 0, 0, allow_small_or_imprecise_dtypes=True))
-    tt(["ta", "tx"], ["tb"], T.tb[:, :], T.ta[:, :], T.tx[:, 64:128], A.add)
+    act(["tx2"], ["u2"], T.txu[:, 0:64], T.tx[:, 128:192])
+    act(["u2", "i16"], ["mt2"], *mask(2))
+    cp(["pr"], ["pru"], T.pru[:, :], T.pr[:, :])
+    ts(["pr"], ["a16"], T.a16[:, :], T.pr[:, 0:4], 16.0, A.mult, 64.0 * r, A.add)
+    fill(["ones"], T.ones[0:1, :], 1.0)
+    for q in range(4):
+        base(0, q)
+    ts(["lb"], ["l2w"], T.l2w[:, :], T.lb[:, 0:64], 16.0, A.mult)
+    cp(["lb"], ["x2"], T.x3[:, 512:576], T.lb[:, 0:64])
+    cp(["tx3"], ["u3"], T.txu[:, 64:128], T.tx[:, 192:256])
+    tt(["l2w", "pru", "lb"], ["x3"], T.x3[:, 0:512], T.l2w[:, :].indirect(T.pru[:, 4:36]), T.lb[:, 64:576], A.add)
+    tolist(["x2", "x3"], "pl0", "x3", 576, "zb")
+    act(["x3", "pru"], ["x4i"], T.x4i[:, :], T.x3[:, 0:512].indirect(T.pru[:, 36:68]))
+    ts(["t3"], ["B3%d" % r], T.sB3[:, o3:o3 + 512], T.t3[:, :], float(C0 + 512 * r), A.subtract)
+    cp(["t12"], ["yg1"], T.o1[:, :], T.t12[:, 4:8])
+    fill(["of1"], T.of12[:, 0:4], 0.0)
+    ts(["lb"], ["of2"], T.of12[:, 4:68], T.lb[:, 0:64], 16.0, A.add)
+    cp(["pl0"], ["La"], T.sB3[:, o3 + 512:o3 + 544], T.pl0[:, 0:32])
+    tt(["pl0", "a16"], ["Lb"], T.sB3[:, o3 + 544:o3 + 548], T.pl0[:, 32:36], T.a16[:, :], A.add)
+    send("B3", ["B3%d" % r, "La", "Lb"])
+    bases(1)
+    for h in range(2):
+        cp(["lt"], ["lt2%d" % h], T.lt2[:, :, 16 * h:16 * h + 16], T.lt[:, h])
+    cp(["tx4"], ["tf"], T.tf[:, :], T.tx[:, 256:384])
+    for u in range(2):
+        op("v", ["lt20", "lt21"], ["lt3%d" % u], lambda: V.transpose(T.lt3[:, 32 * u:32 * u + 32], T.lt2[:, u, :]))
+    tolist(["x4i"], "pl1", "x4i", 512, "zb")
+    swap(["tf"], "pl0", "tf", 0)
+    swap(["tf"], "pl0", "tf", 64)
+    widen("B3", r)
+    ts(["tx0"], ["ta"], T.ta[:, :], T.tx[:, 0:64], 16.0, A.mult)
+    for u in range(2):
+        cp(["lt3%d" % u], ["ltu%d" % u], T.ltu[:, u:64:2], T.lt3[:, 32 * u:32 * u + 32])
+    LT = ["ltu0", "ltu1"]
+    act(["u3", "i16"], ["mt3"], *mask(3))
+    tt(["ta", "tx0"], ["tb"], T.tb[:, :], T.ta[:, :], T.tx[:, 64:128], A.add)
+    ts(["t4"], ["B4%d" % r], slot(T, "B4", r), T.t4[:, :], float(C0 + 2048 + 512 * r), A.subtract)
+    hand("B4", ["B4%d" % r])
+    count(["nat"], T.nat[:, :], [[1, 256]], 0, 0)
+    cp(LT + ["i16"], ["m4"], T.m4[:, :], T.i16[:, :].indirect(T.ltu[:, 0:32]))
+    act(["pl0"], ["u45"], T.txu[:, 128:256], T.pl0[:, 0:128])
+    act(["u45", "i16"], ["mt4"], *mask(4))
     lists(r)
     cp(["pl1"], ["i4"], T.i4[:, :], T.pl1[:, 0:32])
     cp(["tb"], ["i01"], T.i01[:, :], T.tb[:, :])
-    cp(["txu", "i16"], ["mt3v"], T.mt[:, 1024:2048], T.i16[:, :].indirect(T.txu[:, 64:128]))
+    ts(["tx0"], ["r0"], T.r0[:, :], T.tx[:, 0:64], 12, A.bitwise_and)
+    for h in range(2):
+        mms(["mt4", "ib"], ["pa%d" % h], [(T["pa%d" % h][:, :], IB, T.mt[:, 2048 + 512 * h:2560 + 512 * h], True, False)])
+    act(LT + ["i16"], ["m5"], T.m5[:, :], T.i16[:, :].indirect(T.ltu[:, 32:64]))
+    cp(["u45", "i16"], ["mt5"], *mask(5, 0, 1024 - K5))
+    deps("y", ["mt4"], [])
     store(["of1", "of2"], T.yf[:, 0:68], T.of12[0:128:16, :])
+    store(["yg1"], T.yg[:, 0:4], T.o1[:, :])
 
     cp(["Sall", "S1"], ["g1"], T.g1[:, :], T.sS[:, :, 0:4])
     for q in range(4):
@@ -303,96 +338,128 @@ def rank_program(g, core, T, topo):
 
     def d3(q):
         act(W2 + ["lst%d" % q], ["g3%d" % q], T.wg[:, G3 + 512 * q:G3 + 512 * q + 512],
-            T.w2[:, :].indirect(T.lst[:, 36 * q:36 * q + 32]), bias=S2 - SH)
+            T.w2[:, :].indirect(T.lst[:, 36 * q:36 * q + 32]), bias=S2)
 
     def g2(q):
         act(W2 + ["lst%d" % q], ["g2%d" % q], T.wg[:, 64 * q:64 * q + 64],
-            T.w2[:, :].indirect(T.lst[:, 36 * q + 32:36 * q + 36]), bias=S2 - SH)
+            T.w2[:, :].indirect(T.lst[:, 36 * q + 32:36 * q + 36]), bias=S2)
 
     def top(name, o, q):
         a = T.wg[:, o + 512 * q:o + 512 * q + 512]
         tt([name + str(q), "pt%d" % q], [name + str(q)], a, a, T["pt%d" % q][:, :], A.max)
 
+    def fails_out(l):
+        op("v", ["fl%d" % l], ["ft%d" % l], lambda: V.transpose(T.ft[:, 32 * l:32 * l + 32], T.fl[:, 32 * l:32 * l + 32]))
+        for h in range(2):
+            store(["ft%d" % l], T.yf[h::2, 580 + 512 * l:1092 + 512 * l], T.ft[:, 32 * l + 16 * h:32 * l + 16 * h + 16])
+
     G23 = ["g2%d" % q for q in range(4)] + ["g3%d" % q for q in range(4)]
     GG = G23 + ["g4%d" % q for q in range(4)]
     w23, wgg = T.wg[:, 0:G4], T.wg[:, 0:GE]
 
-    tt(W2 + ["i4", "m4"], ["xf4"], T.xf4[:, :], T.w2[:, :].indirect(T.i4[:, :]), T.m4[:, :], A.mult)
-    d3(r); g2(r)
-    tolist([], "pl2", "xf4", 512, "zh")
-    lists(direct)
-    ts(["g1"], ["l1a"], T.l1a[:, :], T.g1[:, :], float(S2 - 32), A.add)
-    d3(direct); g2(direct)
-    act(["io", "l1a"], ["n2"], T.n2[:, :], T["io"][:, :].indirect(T.l1a[:, :]), scale=1.0 / 16)
-    tt(W2 + ["i01", "mt2"], ["xh0"], T.xh[:, 0:512], T.w2[:, :].indirect(T.i01[:, 0:32]), T.mt[:, 0:512], A.mult)
-    ts(["pl2"], ["F%d" % r], slot(T, "F", r), T.pl2[:, 0:32], float(S2 - 32), A.add)
-    send("F", ["F%d" % r], True)
-    send("F", [], False)
-    widen("B3", direct)
-    tt(W2 + ["i01", "mt2"], ["xh"], T.xh[:, 512:1024], T.w2[:, :].indirect(T.i01[:, 32:64]), T.mt[:, 512:1024], A.mult)
-    tolist(["xh0"], "pl3", "xh", 1024, "zh")
-    lists(c1); lists(c2)
-    widen("B3", c1); widen("B3", c2)
-    d3(c1); d3(c2); g2(c1); g2(c2)
-    top("g3", G3, r); top("g3", G3, direct)
-    ts(["pl3"], ["i3"], T.i3[:, :], T.pl3[:, 0:64], float(S2 - 32), A.add)
-    ts(["pl3"], ["mx"], T.mx[:, :], T.pl3[:, 0:64], float(S2 - SH), A.add)
-    ts(["pl2"], ["fl4"], T.fl[:, 0:32], T.pl2[:, 0:32], float(S2), A.add)
-    top("g3", G3, c1); top("g3", G3, c2)
-    widen("B4", r); widen("B4", direct)
+    def look(R, x, win, idx, t, h):
+        o = 1024 * (t - 2) + 512 * h
+        tt(R + [idx, "mt%d" % t], [x + str(h)], T[x][:, 512 * h:512 * h + 512], win.indirect(T[idx][:, 32 * h:32 * h + 32]),
+           T.mt[:, o:o + 512], A.mult)
 
-    tt(G23 + ["i3", "mt3v"], ["xa"], T.xa[:, :], w23.indirect(T.i3[:, :]), T.mt[:, 1024:2048], A.mult)
+    tt(W2 + ["i4", "m4"], ["xf4"], T.xf4[:, :], T.w2[:, :].indirect(T.i4[:, :]), T.m4[:, :], A.mult)
+    d3(r); lists(direct); g2(r)
+    tolist(["xf4"], "pl0", "xf4", 512, "zh")
+    look(W2, "xh", T.w2[:, :], "i01", 2, 0)
+    d3(direct)
+    act(["pl0"], ["F%d" % r], slot(T, "F", r), T.pl0[:, 0:32], bias=S2 - 32)
+    lists(c1); lists(c2); g2(direct)
+    send("F", ["F%d" % r])
+    straight("B4")
+    widen("B3", direct)
+    look(W2, "xh", T.w2[:, :], "i01", 2, 1)
+    widen("B3", c1); widen("B3", c2)
+    tolist(["xh0", "xh1"], "pl1", "xh", 1024, "zh")
+    d3(c1); d3(c2)
+    act(["pl1"], ["i3"], T.i3[:, :], T.pl1[:, 0:64], bias=S2 - 32)
+    g2(c1); g2(c2)
+    for h in range(2):
+        act(["r0"], ["crt%d" % h], T.crt[:, h:64:2], T.r0[:, 32 * h:32 * h + 32], bias=C0 + 2048 - LIFT, scale=128.0)
+    for q in order:
+        top("g3", G3, q)
+        base(1, q)
+        if q == r:
+            widen("B4", q)
+    store(["g2%d" % r], T.yg[:, 4:68], T.wg[:, 64 * r:64 * r + 64])
+    store(["g3%d" % r], T.yg[:, 68:580], T.wg[:, G3 + 512 * r:G3 + 512 * r + 512])
+
     for q in order:
         act(G23 + ["F%d" % q], ["g4%d" % q], T.wg[:, G4 + 512 * q:G4 + 512 * q + 512], w23.indirect(slot(T, "F", q)))
-    act(["n2", "i01"], ["xs"], T.xs[:, :], T.n2[:, :].indirect(T.i01[:, :]))
-    mask(5)
-    tolist([], "pl0", "xa", 1024, "zf")
-    cp(LT + ["i16"], ["m5"], T.m5[:, :], T.i16[:, :].indirect(T.ltu[:, 64:96]))
+    for h in range(2):
+        look(G23, "xa", w23, "i3", 3, h)
+        halflist(["xa%d" % h], "pl0", "xa", h, "zf")
     tt(["g4%d" % r, "pru", "m5"], ["xb"], T.xb[:, :],
        T.wg[:, G4 + 512 * r:G4 + 512 * r + 512].indirect(T.pru[:, 68:100]), T.m5[:, :], A.mult)
-    widen("B4", c1); widen("B4", c2)
-    ts(["pl0"], ["i4g"], T.i4g[:, :], T.pl0[:, 0:64], float(SH - 32), A.add)
-    tt(["pl0", "mx"], ["mx"], T.mx[:, :], T.pl0[:, 0:64], T.mx[:, :], A.max)
-    tolist([], "pl3", "xs", 1024, "zb")
+    mms(["xb", "z2"], ["pl1"], [(T.pl1[:, 0:64], T.z2[:, 7 - i:135 - i], T.xb[:, i:512:8], i == 0, i == 7) for i in range(8)])
+    for q in order[1:]:
+        widen("B4", q)
+    ts(["g1"], ["l1a"], T.l1a[:, :], T.g1[:, :], float(S2 - 32), A.add)
+    ts(["F%d" % r], ["fl0"], T.fl[:, 0:32], slot(T, "F", r), 32.0, A.add)
+    cp(["nat", "l1a"], ["n2"], T.n2[:, :], T.nat[:, :].indirect(T.l1a[:, :]))
+    for u in range(2):
+        ts(["pl0"], ["i4g%d" % u], T.i4g[:, 32 * u:32 * u + 32], T.pl0[:, u:64:2], 32.0, A.subtract)
+    fails_out(0)
+    I4 = ["i4g0", "i4g1"]
+    ts(I4, ["ip"], T.ip[:, :], T.i4g[:, :], float(G4 - PAD), A.subtract)
 
-    tt(GG + ["i4g", "mt4"], ["xc"], T.xc[:, :], wgg.indirect(T.i4g[:, :]), T.mt[:, 2048:3072], A.mult)
-    act(["g2%d" % r], ["yg2"], T.oyg[:, 4:68], T.wg[:, 64 * r:64 * r + 64], bias=SH)
-    act(["g3%d" % r], ["yg3"], T.oyg[:, 68:580], T.wg[:, G3 + 512 * r:G3 + 512 * r + 512], bias=SH)
-    store(["yg1", "yg2", "yg3"], T.yg[:, 0:580], T.oyg[:, 0:580])
-    tolist([], "pl2", "xc", 1024, "zf")
-    tolist([], "pl1", "xb", 512, "zf")
+    tt(GG + I4 + ["mt4"], ["xc"], T.xc[:, :], wgg.indirect(T.i4g[:, :]), T.mt[:, 2048:3072], A.mult)
+    B4 = ["B4%d" % q for q in range(4)] + ["pad"]
+    for h in range(2):
+        act(B4 + ["ip"], ["xp%d" % h], T.xp[:, 512 * h:512 * h + 512], T.sB4[:, :].indirect(T.ip[:, 32 * h:32 * h + 32]),
+            scale=1.0 / 1024)
+        if h == 0:
+            act(["pl1", "lo"], ["fa"], T.fa[:, :], T.pl1[:, 0:64:2], scale=T.lo[:, :])
+            act(["pl1", "hi"], ["fb"], T.fb[:, :], T.pl1[:, 1:64:2], scale=T.hi[:, :])
+        else:
+            tolist(["xc"], "pl0", "xc", 1024, "zf", range(6))
+        mms(["xp%d" % h, "ib"], ["pa%d" % h], [(T["pa%d" % h][:, :], IB, T.xp[:, 512 * h:512 * h + 512], False, True)])
+    tolist(["xc"], "pl0", "xc", 1024, "zf", range(6, 16))
+    for h in range(2):
+        act(["pa%d" % h], ["xy%d" % h], T.xy[:, 512 * h:512 * h + 512], T["pa%d" % h][:, :], bias=LIFT - 1024, scale=1024.0,
+            f=AF.Relu)
+    ts(I4, ["a3"], T.a3[:, :], T.i4g[:, :], 32.0, A.add)
+    tt(["fa", "fb"], ["fl1"], T.fl[:, 32:64], T.fa[:, :], T.fb[:, :], A.add)
     deps("v", ["xc"], [])
     for q in order:
         top("g4", G4, q)
-    act(["g4%d" % r], ["yg4"], T.oyg[:, 580:1092], T.wg[:, G4 + 512 * r:G4 + 512 * r + 512], bias=SH)
-    store(["yg4"], T.yg[:, 580:1092], T.oyg[:, 580:1092])
-    act(["n2", "lst%d" % r], ["of3"], T.of3[:, :], T.n2[:, :].indirect(T.lst[:, 36 * r:36 * r + 32]), bias=32.0, scale=16.0)
-    store(["of3"], T.yf[:, 68:580], T.of3[0:128:16, :])
-    ts(["pl2"], ["i5"], T.i5[:, :], T.pl2[:, 0:64], float(SH - 32), A.add)
-    tt(["pl2", "mx"], ["mx"], T.mx[:, :], T.pl2[:, 0:64], T.mx[:, :], A.max)
+        if q == r:
+            store(["g4%d" % r], T.yg[:, 580:1092], T.wg[:, G4 + 512 * r:G4 + 512 * r + 512])
+    act(["u45", "i16"], ["mt5a"], *mask(5, 1024 - K5, 1024))
+    act(["fl1"], ["if5"], T.if5[:, :], T.fl[:, 32:64], bias=-32)
+    for h in range(2):
+        halflist(["xy%d" % h], "pa0", "xy", h, "zh", last=False)
+    mms(["crt0", "crt1", "ib"], ["pa0"], [(T.pa0[:, 0:64], IB, T.crt[:, :], False, True)])
+    ts(["pl0"], ["i5"], T.i5[:, :], T.pl0[:, 0:64], 32.0, A.subtract)
+    tt(["pl0", "a3"], ["mp"], T.mp[:, :], T.pl0[:, 0:64], T.a3[:, :], A.max)
+    swap(["mp"], "pa1", "mp", 0)
+    act(GG + ["if5"], ["yg5"], T.o5[:, :], wgg.indirect(T.if5[:, :]))
+    store(["yg5"], T.yg[:, 1092:1604], T.o5[:, :])
+    act(["n2", "i01"], ["xs"], T.xs[:, :], T.n2[:, :].indirect(T.i01[:, :]), bias=2.0, scale=1.0 / 16)
 
-    tt(GG + ["i5", "mt5"], ["xa"], T.xa[:, :], wgg.indirect(T.i5[:, :]), T.mt[:, 3072:4096], A.mult)
-    tolist([], "pl0", "xa", 1024, "zf")
-    ts(["pl3"], ["uc"], T.uc[:, :], T.pl3[:, 0:64], 32.0, A.add)
-    ts(["mx"], ["mx"], T.mx[:, :], T.mx[:, :], float(SH), A.add)
-    ts(["pl1"], ["if5"], T.if5[:, :], T.pl1[:, 0:32], float(SH - 32), A.add)
-    ts(["pl1"], ["fl5"], T.fl[:, 32:64], T.pl1[:, 0:32], float(SH), A.add)
-    act(GG + ["if5"], ["yg5"], T.oyg[:, 1092:1604], wgg.indirect(T.if5[:, :]), bias=SH)
-    op("v", ["fl4", "fl5"], ["ft"], lambda: V.transpose(T.ft[:, :], T.fl[:, :]))
-    for l in range(2):
-        for h in range(2):
-            store(["ft"], T.yf[h::2, 580 + 512 * l:1092 + 512 * l], T.ft[:, 32 * l + 16 * h:32 * l + 16 * h + 16])
-    store(["yg5"], T.yg[:, 1092:1604], T.oyg[:, 1092:1604])
-    tt(GG + ["i4g", "mt4"], ["xh", "xh0"], T.xh[:, :], wgg.indirect(T.i4g[:, :]), T.mt[:, 2048:3072], A.mult)
-    tolist([], "pl2", "xh", 1024, "zh")
-    tt(["uc", "mx"], ["mx"], T.mx[:, :], T.uc[:, :], T.mx[:, :], A.max)
-    ts(["pl0"], ["oyl"], T.oyl[:, :], T.pl0[:, 0:64], float(SH), A.add)
-    store(["oyl"], T.yl[:, :], T.oyl[:, :])
-    tt(["oyl", "mx"], ["mx"], T.mx[:, :], T.oyl[:, :], T.mx[:, :], A.max)
-    ts(["pl2"], ["va"], T.va[:, :], T.pl2[:, 0:64], 0.0, A.is_ge, float(SH), A.mult)
-    tt(["pl2", "va"], ["vb"], T.vb[:, :], T.pl2[:, 0:64], T.va[:, :], A.add)
-    tt(["vb", "mx"], ["oym"], T.oym[:, :], T.vb[:, :], T.mx[:, :], A.max)
-    store(["oym"], T.ym[:, :], T.oym[:, :])
+    for h in range(2):
+        look(GG + ["mt5a"] * h, "xa", wgg, "i5", 5, h)
+        halflist(["xa%d" % h], "pl0", "xa", h, "zf")
+    tolist(["xs"], "pl1", "xs", 1024, "zh")
+    act(["n2", "lst%d" % r], ["of3"], T.of3[:, :], T.n2[:, :].indirect(T.lst[:, 36 * r:36 * r + 32]), bias=32.0)
+    store(["of3"], T.yf[:, 68:580], T.of3[0:128:16, :], "a")
+    fails_out(1)
+    ts(["i3"], ["mx"], T.mx[:, :], T.i3[:, :], 32.0, A.add)
+    tt(["pa0", "crt0", "crt1"], ["va"], T.va[:, :], T.pa0[:, 0:64], T.crt[:, :], A.is_gt)
+    tt(["pa1", "mx"], ["mx"], T.mx[:, :], T.pa1[:, 0:64], T.mx[:, :], A.max)
+    tt(["pa0", "va"], ["vb"], T.vb[:, :], T.pa0[:, 0:64], T.va[:, :], A.mult)
+    for h in range(2):
+        tt(["vb", "mx"], ["mx%d" % h], T.mx[:, 32 * h:32 * h + 32], T.vb[:, h:64:2], T.mx[:, 32 * h:32 * h + 32], A.max)
+    for h in range(2):
+        cp(["pl0"], ["oyl%d" % h], T.oyl[:, 32 * h:32 * h + 32], T.pl0[:, h:64:2])
+    store(["oyl0", "oyl1"], T.yl[:, :], T.oyl[:, :])
+    tt(["oyl0", "oyl1", "mx0", "mx1"], ["va"], T.va[:, :], T.oyl[:, :], T.mx[:, :], A.max)
+    tt(["va", "pl1"], ["oym"], T.oym[:, :], T.pl1[:, 0:64], T.va[:, :], A.max)
+    store(["oym"], T.ym[:, :], T.oym[:, :], "a")
 
     g.wait_ge(T.sem.snd, nsent[0])
     for e in ("v", "a", "p", "g"):

from concourse.bass import DstId, RemoteDMATransfer
from concourse.mybir import AluOpType as A, ActivationFunctionType as AF

S2 = 1184
C0 = 2592
WS, WB, NB, WF, PAD = 68, 552, 548, 32, 16
G3, G4, GE = 256, 2304, 4352
K5 = 256
LIFT = 288

F32, BF, F16, I32, U16 = "float32", "bfloat16", "float16", "int32", "uint16"
SB = {
    I32: dict(t12=72, t3=512, t4=512, pr=100, lb=576, lt3=64, tx=384, dm=144, p4=4, sh8=8, t16=16, ca=4, r0=64),
    U16: dict(pru=100, ltu=64, txu=256, i01=64, cl=4, l1=4, l1a=16, i4=32, sF=4 * WF, lst=144,
              i3=64, i4g=64, ip=64, i5=64, if5=32),
    BF: dict(nat=256, i16=16, zb=144, iw=144, crow=1024, ones=512, l2w=64, x3=576, x4i=512, m4=512, m5=512, mt=4096,
             sB3=4 * WB, sB4=PAD + 2048, n2=256, xp=1024, crt=64),
    F16: dict(zh=144, xf4=512, xh=1024, xs=1024, xy=1024),
    F32: dict(zf=144, z2=136, sw=512, lo=1, hi=1, g1=16, a16=4, ta=64, tb=64, tf=128, w2=256, wg=GE,
              xa=1024, xb=512, xc=1024, a3=64, mp=64, mx=64, va=64, vb=64, oyl=64, oym=64, fa=32, fb=32, fl=64, ft=64,
              o1=4, o5=512, of12=68, of3=512),
}
SCRATCH = {n: ("sbuf", [128, w], d) for d, b in SB.items() for n, w in b.items()}
SCRATCH.update(lt=("sbuf", [128, 2, 2, 16], I32), lt2=("sbuf", [128, 2, 32], I32), sS=("sbuf", [128, 4, WS + 4], F16))
BANKS = ["pt0", "pt1", "pt2", "pt3", "pa0", "pa1", "pl0", "pl1"]
SCRATCH.update({b: ("psum", [128, 512], F32) for b in BANKS})
SEMAPHORES = (["cv", "ca", "cp", "cg", "l12", "lpr", "llb", "llt", "lt3", "lt4", "lx0", "lx2", "lx3", "lx4", "out", "snd", "aS"]
              + ["a%s%d" % (k, q) for k in ("B3", "B4", "F") for q in range(4)])


def routes(T, topo, rank):
    core = T.cores[rank]
    others = [q for q in range(len(T.cores)) if q != rank]
    direct = [q for q in others if topo.may_write(core, T.cores[q])][0]
    cross = sorted((q for q in others if q != direct), key=lambda q: topo.host(T.cores[q]) != topo.host(core))
    able = [h for h in topo.cores_of(core) if h != core and topo.may_write(h, T.cores[cross[0]])]
    near = [h for h in able if topo.die(h) == topo.die(core)]
    far = [h for h in able if h not in near]
    off = topo.engines(core, T.cores[direct])
    on = [e for e in topo.engines(core, near[0]) if e not in off]
    return direct, cross, [(near[0], on, ("S", "B3", "F"), cross[:1]), (far[0], off, ("S", "B3", "F"), cross[1:]),
                           (far[1], on, ("B4",), cross)]


def slot(T, kind, q):
    if kind == "S":
        return T.sS[:, q, 0:WS]
    o, w, n = {"B3": (0, WB, NB), "B4": (PAD, 512, 512), "F": (0, WF, WF)}[kind]
    return T["s" + kind][:, o + w * q:o + w * q + n]


def asem(T, kind, q):
    return T.sem["aS"] if kind == "S" else T.sem["a%s%d" % (kind, q)]


def bits(engs):
    return sum(1 << e for e in engs)


def helper_program(g, core, T, topo, rank, engs, kinds, ranks):
    sent = 0
    for kind in kinds:
        g.wait_ge(asem(T, kind, rank), len(engs))
        for q in ranks:
            rid, pid = topo.addr(T.cores[q], core)
            g.remote_dma(slot(T, kind, rank), slot(T, kind, rank), asem(T, kind, rank), T.sem.snd, pid, rid,
                         topo.mask(core, T.cores[q]))
            sent += len(topo.engines(core, T.cores[q]))
    g.wait_ge(T.sem.snd, sent)


def rank_program(g, core, T, topo):
    r = T.rank_of(core)
    if r is None:
        for q in range(len(T.cores)):
            for h, engs, kinds, ranks in routes(T, topo, q)[2]:
                if h == core:
                    helper_program(g, core, T, topo, q, engs, kinds, ranks)
        return

    direct, (c1, c2), helpers = routes(T, topo, r)
    off = topo.engines(core, T.cores[direct])
    order = [r, direct, c1, c2]
    nin = len(off)

    Q = {"v": g.vector, "a": g.scalar, "p": g.tensor, "g": g, "y": g.sync}
    SEM = {"v": "cv", "a": "ca", "p": "cp", "g": "cg"}
    cnt = {"v": 0, "a": 0, "p": 0, "g": 0}
    known = {e: {} for e in Q}
    lastw, readers, bank = {}, {}, {}

    def need(e, tok):
        sem, n, _src, seen = tok
        if known[e].get(sem, 0) < n:
            Q[e].wait_ge(T.sem[sem], n)
            known[e][sem] = n
        for s, m in seen.items():
            if known[e].get(s, 0) < m:
                known[e][s] = m

    def deps(e, R, W):
        toks = [lastw[x] for x in R if x in lastw]
        for x in W:
            toks += [t for t in readers.get(x, []) + ([lastw[x]] if x in lastw else []) if t[2] != e]
        toks += [bank[x] for x in R + W if x in bank and bank[x][2] != e]
        toks.sort(key=lambda t: -t[1])
        for t in toks:
            need(e, t)

    def op(e, R, W, fn):
        deps(e, R, W)
        ins = fn()
        cnt[e] += 1
        ins.then_inc(T.sem[SEM[e]], 1)
        tok = (SEM[e], cnt[e], e, dict(known[e]))
        for x in R:
            readers.setdefault(x, []).append(tok)
        for x in W:
            lastw[x] = tok
            readers[x] = []
        for x in R + W:
            if x in BANKS:
                bank[x] = tok

    def ext(x, sem, n):
        lastw[x] = (sem, n, None, {})

    V, ACT, PE = g.vector, g.scalar, g.tensor
    IB = T.iw[:, 8:136]

    def ts(R, W, out, in0, s1, op0, s2=None, op1=None):
        if op1 is None:
            op("v", R, W, lambda: V.tensor_scalar(out, in0, s1, None, op0))
        else:
            op("v", R, W, lambda: V.tensor_scalar(out, in0, s1, s2, op0, op1))

    def tt(R, W, out, in0, in1, o):
        op("v", R, W, lambda: V.tensor_tensor(out, in0, in1, o))

    def cp(R, W, out, in_):
        op("v", R, W, lambda: V.tensor_copy(out, in_))

    def fill(W, out, c):
        op("v", [], W, lambda: V.memset(out, c))

    def act(R, W, out, in_, bias=0.0, scale=1.0, f=None):
        f = f or (AF.Copy if bias == 0.0 else AF.Identity)
        op("a", R, W, lambda: ACT.activation(out, in_, f, bias=float(bias), scale=scale))

    def count(W, out, pattern, start, step):
        op("g", [], W, lambda: g.iota(out, pattern, start, step, allow_small_or_imprecise_dtypes=True))

    def mms(R, W, calls):
        def run():
            for c in calls:
                ins = PE.matmul(*c)
            return ins
        op("p", R, W, run)

    def tolist(R, b, x, n, z, rows=range(16)):
        mms(R + [z], [b], [(T[b][:, 0:n // 16], T[z][:, 15 - i:143 - i], T[x][:, i:n:16], i == 0, i == 15)
                           for i in rows])

    def halflist(R, b, x, h, z, last=True):
        mms(R + [z], [b], [(T[b][:, 0:64], T[z][:, 15 - 8 * h - i:143 - 8 * h - i], T[x][:, 512 * h + i:512 * h + 512:8],
                            h == 0 and i == 0, last and h == 1 and i == 7) for i in range(8)])

    def swap(R, b, x, o):
        mms(R + ["sw"], [b], [(T[b][:, o + 32 * u:o + 32 * u + 32], T.sw[:, 128 * (2 * u + h):128 * (2 * u + h) + 128],
                               T[x][:, o + 32 * h:o + 32 * h + 32], h == 0, h == 1) for u in range(2) for h in range(2)])

    def bases(l):
        count(["crow%d" % l], T.crow[0:1, 512 * l:512 * l + 512], [[512, 4], [0, 128]], C0 + 2048 * l, 0)

    def base(l, q):
        k = 4 * l + q
        mms(["crow%d" % l, "ones"], ["pt%d" % q],
            [(T["pt%d" % q][:, :], T.crow[0:1, 128 * k:128 * k + 128], T.ones[0:1, :], True, False)])

    def widen(kind, q):
        mms([kind + str(q), "ib"], ["pt%d" % q],
            [(T["pt%d" % q][:, :], IB, slot(T, kind, q) if kind == "B4" else T.sB3[:, WB * q:WB * q + 512], False, True)])

    nsent = [0]

    def hand(kind, R):
        deps("g", R, [])
        src, trs = slot(T, kind, r), []
        for h, engs, kinds, _ranks in helpers:
            if kind in kinds:
                rid, pid = topo.addr(h, core)
                trs.append(RemoteDMATransfer(dst_ids=[DstId(rid=rid, pnc=pid)], dma_engine_mask=bits(engs),
                                             remote_sem=asem(T, kind, r), src=src, dst=src))
                nsent[0] += len(engs)
        g.remote_dma_fused(trs, local_sem=T.sem.snd)

    def straight(kind):
        rid, pid = topo.addr(T.cores[direct], core)
        g.remote_dma(slot(T, kind, r), slot(T, kind, r), asem(T, kind, r), T.sem.snd, pid, rid, bits(off))
        nsent[0] += len(off)

    def send(kind, R):
        hand(kind, R)
        straight(kind)

    nout = [0]

    def store(R, out, in_, e="y"):
        deps(e, R, [])
        Q[e].dma_start(out, in_).then_inc(T.sem.out, 16)
        nout[0] += 16

    def load(e, x, sem, pairs_):
        for out, in_ in pairs_:
            Q[e].dma_start(out, in_).then_inc(T.sem[sem], 16)
        ext(x, sem, 16 * len(pairs_))

    def text(t):
        return T.tx[:, 64 * t:64 * t + 64], T.txt[:, 1024 * t:1024 * t + 1024]

    fill(["lb0"], T.lb[:, :], 0)
    load("y", "t12", "l12", [(T.t12[:, 4:72], T.tri[:, 0:68])])
    load("y", "tx2", "lx2", [text(2)])
    load("y", "pr", "lpr", [(T.pr[:, :], T.par[:, :])])
    load("y", "tx3", "lx3", [text(3)])
    deps("a", ["lb0"], [])
    load("a", "tx4", "lx4", [text(4), text(5)])
    load("a", "lt", "llt", [(T.lt[:, h], T.let[h::2, 576:1600]) for h in range(2)])
    load("a", "tx0", "lx0", [text(0), text(1)])
    deps("y", ["lb0"], [])
    load("y", "lb", "llb", [(T.lb[0:128:16, :], T.let[:, 0:576])])
    load("y", "t3", "lt3", [(T.t3[:, :], T.tri[:, 68:580])])
    load("y", "t4", "lt4", [(T.t4[:, :], T.tri[:, 580:1092])])
    ext("Sall", "aS", 3 * nin)
    for q in order[1:]:
        for kind in ("B3", "B4", "F"):
            ext(kind + str(q), "a%s%d" % (kind, q), nin)
        ext("L%d" % q, "aB3%d" % q, nin)

    op("g", [], ["p4"], lambda: g.iota(T.p4[:, :], [[0, 4]], 0, 1))
    op("g", [], ["dm"], lambda: g.iota(T.dm[:, :], [[1, 144]], -8, -1))
    bases(0)
    fill(["zb0"], T.zb[:, :], 0.0)
    ts(["p4"], ["ca"], T.ca[:, :], T.p4[:, :], 15, A.bitwise_and)
    ts(["dm"], ["ib"], T.iw[:, :], T.dm[:, :], 0.0, A.is_equal)
    ts(["ca"], ["lo"], T.lo[:, :], T.ca[:, 0:1], 8.0, A.is_lt)
    ts(["ca"], ["hi"], T.hi[:, :], T.ca[:, 0:1], 8.0, A.is_ge)
    ts(["dm"], ["sh8"], T.sh8[:, :], T.dm[:, 23:144:16], 4, A.arith_shift_right)
    ts(["dm"], ["t16"], T.t16[:, :], T.dm[:, 8:24], 15, A.bitwise_and)
    fill(["z20"], T.z2[:, :], 0.0)
    ts(["sh8", "zb0"], ["zb"], T.zb[:, 15:143:16], T.sh8[:, :], 0.0, A.is_equal)
    ts(["t16"], ["i16"], T.i16[:, :], T.t16[:, :], 0.0, A.is_equal)
    for o in (7, 15):
        ts(["sh8", "z20"], ["z2"], T.z2[:, o:o + 120:16], T.sh8[:, :], 0.0, A.is_equal)
    cp(["ca"], ["cl"], T.cl[:, :], T.ca[:, :])
    for u in range(2):
        for h in range(2):
            k, o = 128 * (2 * u + h), 8 - 8 * (h - u)
            act(["ib", "lo", "hi"], ["sw"], T.sw[:, k:k + 128], T.iw[:, o:o + 128], scale=(T.lo, T.hi)[u][:, :])
    act(["zb"], ["zh"], T.zh[:, :], T.zb[:, :])
    act(["zb"], ["zf"], T.zf[:, :], T.zb[:, :])

    ts(["t12"], ["l1"], T.l1[:, :], T.t12[:, 4:8], float(32 + 64 * r), A.subtract)
    ts(["t12"], ["S1"], T.sS[:, r, 0:4], T.t12[:, 4:8], float(S2), A.subtract)
    ts(["t12", "l1"], ["S2"], T.sS[:, r, 4:WS], T.t12[:, 8:72].indirect(T.l1[:, :]), float(S2), A.subtract)
    send("S", ["S1", "S2"])
    fill(["pad"], T.sB4[:, 0:PAD], -32768.0)

    o3 = WB * r

    def mask(t, a=0, b=1024):
        o = 64 * (t - 2)
        return T.mt[:, 16 * o + a:16 * o + b], T.i16[:, :].indirect(T.txu[:, o + a // 16:o + b // 16])

    def lists(q):
        R = ["La", "Lb"] if q == r else ["L%d" % q]
        (cp if q == r else act)(R, ["lst%d" % q], T.lst[:, 36 * q:36 * q + 36], T.sB3[:, WB * q + 512:WB * q + NB])

    act(["tx2"], ["u2"], T.txu[:, 0:64], T.tx[:, 128:192])
    act(["u2", "i16"], ["mt2"], *mask(2))
    cp(["pr"], ["pru"], T.pru[:, :], T.pr[:, :])
    ts(["pr"], ["a16"], T.a16[:, :], T.pr[:, 0:4], 16.0, A.mult, 64.0 * r, A.add)
    fill(["ones"], T.ones[0:1, :], 1.0)
    for q in range(4):
        base(0, q)
    ts(["lb"], ["l2w"], T.l2w[:, :], T.lb[:, 0:64], 16.0, A.mult)
    cp(["lb"], ["x2"], T.x3[:, 512:576], T.lb[:, 0:64])
    cp(["tx3"], ["u3"], T.txu[:, 64:128], T.tx[:, 192:256])
    tt(["l2w", "pru", "lb"], ["x3"], T.x3[:, 0:512], T.l2w[:, :].indirect(T.pru[:, 4:36]), T.lb[:, 64:576], A.add)
    tolist(["x2", "x3"], "pl0", "x3", 576, "zb")
    act(["x3", "pru"], ["x4i"], T.x4i[:, :], T.x3[:, 0:512].indirect(T.pru[:, 36:68]))
    ts(["t3"], ["B3%d" % r], T.sB3[:, o3:o3 + 512], T.t3[:, :], float(C0 + 512 * r), A.subtract)
    cp(["t12"], ["yg1"], T.o1[:, :], T.t12[:, 4:8])
    fill(["of1"], T.of12[:, 0:4], 0.0)
    ts(["lb"], ["of2"], T.of12[:, 4:68], T.lb[:, 0:64], 16.0, A.add)
    cp(["pl0"], ["La"], T.sB3[:, o3 + 512:o3 + 544], T.pl0[:, 0:32])
    tt(["pl0", "a16"], ["Lb"], T.sB3[:, o3 + 544:o3 + 548], T.pl0[:, 32:36], T.a16[:, :], A.add)
    send("B3", ["B3%d" % r, "La", "Lb"])
    bases(1)
    for h in range(2):
        cp(["lt"], ["lt2%d" % h], T.lt2[:, :, 16 * h:16 * h + 16], T.lt[:, h])
    cp(["tx4"], ["tf"], T.tf[:, :], T.tx[:, 256:384])
    for u in range(2):
        op("v", ["lt20", "lt21"], ["lt3%d" % u], lambda: V.transpose(T.lt3[:, 32 * u:32 * u + 32], T.lt2[:, u, :]))
    tolist(["x4i"], "pl1", "x4i", 512, "zb")
    swap(["tf"], "pl0", "tf", 0)
    swap(["tf"], "pl0", "tf", 64)
    widen("B3", r)
    ts(["tx0"], ["ta"], T.ta[:, :], T.tx[:, 0:64], 16.0, A.mult)
    for u in range(2):
        cp(["lt3%d" % u], ["ltu%d" % u], T.ltu[:, u:64:2], T.lt3[:, 32 * u:32 * u + 32])
    LT = ["ltu0", "ltu1"]
    act(["u3", "i16"], ["mt3"], *mask(3))
    tt(["ta", "tx0"], ["tb"], T.tb[:, :], T.ta[:, :], T.tx[:, 64:128], A.add)
    ts(["t4"], ["B4%d" % r], slot(T, "B4", r), T.t4[:, :], float(C0 + 2048 + 512 * r), A.subtract)
    hand("B4", ["B4%d" % r])
    count(["nat"], T.nat[:, :], [[1, 256]], 0, 0)
    cp(LT + ["i16"], ["m4"], T.m4[:, :], T.i16[:, :].indirect(T.ltu[:, 0:32]))
    act(["pl0"], ["u45"], T.txu[:, 128:256], T.pl0[:, 0:128])
    act(["u45", "i16"], ["mt4"], *mask(4))
    lists(r)
    cp(["pl1"], ["i4"], T.i4[:, :], T.pl1[:, 0:32])
    cp(["tb"], ["i01"], T.i01[:, :], T.tb[:, :])
    ts(["tx0"], ["r0"], T.r0[:, :], T.tx[:, 0:64], 12, A.bitwise_and)
    for h in range(2):
        mms(["mt4", "ib"], ["pa%d" % h], [(T["pa%d" % h][:, :], IB, T.mt[:, 2048 + 512 * h:2560 + 512 * h], True, False)])
    act(LT + ["i16"], ["m5"], T.m5[:, :], T.i16[:, :].indirect(T.ltu[:, 32:64]))
    cp(["u45", "i16"], ["mt5"], *mask(5, 0, 1024 - K5))
    deps("y", ["mt4"], [])
    store(["of1", "of2"], T.yf[:, 0:68], T.of12[0:128:16, :])
    store(["yg1"], T.yg[:, 0:4], T.o1[:, :])

    cp(["Sall", "S1"], ["g1"], T.g1[:, :], T.sS[:, :, 0:4])
    for q in range(4):
        tt(["g1", "S2", "cl"], ["w2%d" % q], T.w2[:, 64 * q:64 * q + 64], T.g1[:, :].indirect(T.cl[:, :]),
           T.sS[:, q, 4:WS], A.max)
    W2 = ["w20", "w21", "w22", "w23"]

    def d3(q):
        act(W2 + ["lst%d" % q], ["g3%d" % q], T.wg[:, G3 + 512 * q:G3 + 512 * q + 512],
            T.w2[:, :].indirect(T.lst[:, 36 * q:36 * q + 32]), bias=S2)

    def g2(q):
        act(W2 + ["lst%d" % q], ["g2%d" % q], T.wg[:, 64 * q:64 * q + 64],
            T.w2[:, :].indirect(T.lst[:, 36 * q + 32:36 * q + 36]), bias=S2)

    def top(name, o, q):
        a = T.wg[:, o + 512 * q:o + 512 * q + 512]
        tt([name + str(q), "pt%d" % q], [name + str(q)], a, a, T["pt%d" % q][:, :], A.max)

    def fails_out(l):
        op("v", ["fl%d" % l], ["ft%d" % l], lambda: V.transpose(T.ft[:, 32 * l:32 * l + 32], T.fl[:, 32 * l:32 * l + 32]))
        for h in range(2):
            store(["ft%d" % l], T.yf[h::2, 580 + 512 * l:1092 + 512 * l], T.ft[:, 32 * l + 16 * h:32 * l + 16 * h + 16])

    G23 = ["g2%d" % q for q in range(4)] + ["g3%d" % q for q in range(4)]
    GG = G23 + ["g4%d" % q for q in range(4)]
    w23, wgg = T.wg[:, 0:G4], T.wg[:, 0:GE]

    def look(R, x, win, idx, t, h):
        o = 1024 * (t - 2) + 512 * h
        tt(R + [idx, "mt%d" % t], [x + str(h)], T[x][:, 512 * h:512 * h + 512], win.indirect(T[idx][:, 32 * h:32 * h + 32]),
           T.mt[:, o:o + 512], A.mult)

    tt(W2 + ["i4", "m4"], ["xf4"], T.xf4[:, :], T.w2[:, :].indirect(T.i4[:, :]), T.m4[:, :], A.mult)
    d3(r); lists(direct); g2(r)
    tolist(["xf4"], "pl0", "xf4", 512, "zh")
    look(W2, "xh", T.w2[:, :], "i01", 2, 0)
    d3(direct)
    act(["pl0"], ["F%d" % r], slot(T, "F", r), T.pl0[:, 0:32], bias=S2 - 32)
    lists(c1); lists(c2); g2(direct)
    send("F", ["F%d" % r])
    straight("B4")
    widen("B3", direct)
    look(W2, "xh", T.w2[:, :], "i01", 2, 1)
    widen("B3", c1); widen("B3", c2)
    tolist(["xh0", "xh1"], "pl1", "xh", 1024, "zh")
    d3(c1); d3(c2)
    act(["pl1"], ["i3"], T.i3[:, :], T.pl1[:, 0:64], bias=S2 - 32)
    g2(c1); g2(c2)
    for h in range(2):
        act(["r0"], ["crt%d" % h], T.crt[:, h:64:2], T.r0[:, 32 * h:32 * h + 32], bias=C0 + 2048 - LIFT, scale=128.0)
    for q in order:
        top("g3", G3, q)
        base(1, q)
        if q == r:
            widen("B4", q)
    store(["g2%d" % r], T.yg[:, 4:68], T.wg[:, 64 * r:64 * r + 64])
    store(["g3%d" % r], T.yg[:, 68:580], T.wg[:, G3 + 512 * r:G3 + 512 * r + 512])

    for q in order:
        act(G23 + ["F%d" % q], ["g4%d" % q], T.wg[:, G4 + 512 * q:G4 + 512 * q + 512], w23.indirect(slot(T, "F", q)))
    for h in range(2):
        look(G23, "xa", w23, "i3", 3, h)
        halflist(["xa%d" % h], "pl0", "xa", h, "zf")
    tt(["g4%d" % r, "pru", "m5"], ["xb"], T.xb[:, :],
       T.wg[:, G4 + 512 * r:G4 + 512 * r + 512].indirect(T.pru[:, 68:100]), T.m5[:, :], A.mult)
    mms(["xb", "z2"], ["pl1"], [(T.pl1[:, 0:64], T.z2[:, 7 - i:135 - i], T.xb[:, i:512:8], i == 0, i == 7) for i in range(8)])
    for q in order[1:]:
        widen("B4", q)
    ts(["g1"], ["l1a"], T.l1a[:, :], T.g1[:, :], float(S2 - 32), A.add)
    ts(["F%d" % r], ["fl0"], T.fl[:, 0:32], slot(T, "F", r), 32.0, A.add)
    cp(["nat", "l1a"], ["n2"], T.n2[:, :], T.nat[:, :].indirect(T.l1a[:, :]))
    for u in range(2):
        ts(["pl0"], ["i4g%d" % u], T.i4g[:, 32 * u:32 * u + 32], T.pl0[:, u:64:2], 32.0, A.subtract)
    fails_out(0)
    I4 = ["i4g0", "i4g1"]
    ts(I4, ["ip"], T.ip[:, :], T.i4g[:, :], float(G4 - PAD), A.subtract)

    tt(GG + I4 + ["mt4"], ["xc"], T.xc[:, :], wgg.indirect(T.i4g[:, :]), T.mt[:, 2048:3072], A.mult)
    B4 = ["B4%d" % q for q in range(4)] + ["pad"]
    for h in range(2):
        act(B4 + ["ip"], ["xp%d" % h], T.xp[:, 512 * h:512 * h + 512], T.sB4[:, :].indirect(T.ip[:, 32 * h:32 * h + 32]),
            scale=1.0 / 1024)
        if h == 0:
            act(["pl1", "lo"], ["fa"], T.fa[:, :], T.pl1[:, 0:64:2], scale=T.lo[:, :])
            act(["pl1", "hi"], ["fb"], T.fb[:, :], T.pl1[:, 1:64:2], scale=T.hi[:, :])
        else:
            tolist(["xc"], "pl0", "xc", 1024, "zf", range(6))
        mms(["xp%d" % h, "ib"], ["pa%d" % h], [(T["pa%d" % h][:, :], IB, T.xp[:, 512 * h:512 * h + 512], False, True)])
    tolist(["xc"], "pl0", "xc", 1024, "zf", range(6, 16))
    for h in range(2):
        act(["pa%d" % h], ["xy%d" % h], T.xy[:, 512 * h:512 * h + 512], T["pa%d" % h][:, :], bias=LIFT - 1024, scale=1024.0,
            f=AF.Relu)
    ts(I4, ["a3"], T.a3[:, :], T.i4g[:, :], 32.0, A.add)
    tt(["fa", "fb"], ["fl1"], T.fl[:, 32:64], T.fa[:, :], T.fb[:, :], A.add)
    deps("v", ["xc"], [])
    for q in order:
        top("g4", G4, q)
        if q == r:
            store(["g4%d" % r], T.yg[:, 580:1092], T.wg[:, G4 + 512 * r:G4 + 512 * r + 512])
    act(["u45", "i16"], ["mt5a"], *mask(5, 1024 - K5, 1024))
    act(["fl1"], ["if5"], T.if5[:, :], T.fl[:, 32:64], bias=-32)
    for h in range(2):
        halflist(["xy%d" % h], "pa0", "xy", h, "zh", last=False)
    mms(["crt0", "crt1", "ib"], ["pa0"], [(T.pa0[:, 0:64], IB, T.crt[:, :], False, True)])
    ts(["pl0"], ["i5"], T.i5[:, :], T.pl0[:, 0:64], 32.0, A.subtract)
    tt(["pl0", "a3"], ["mp"], T.mp[:, :], T.pl0[:, 0:64], T.a3[:, :], A.max)
    swap(["mp"], "pa1", "mp", 0)
    act(GG + ["if5"], ["yg5"], T.o5[:, :], wgg.indirect(T.if5[:, :]))
    store(["yg5"], T.yg[:, 1092:1604], T.o5[:, :])
    act(["n2", "i01"], ["xs"], T.xs[:, :], T.n2[:, :].indirect(T.i01[:, :]), bias=2.0, scale=1.0 / 16)

    for h in range(2):
        look(GG + ["mt5a"] * h, "xa", wgg, "i5", 5, h)
        halflist(["xa%d" % h], "pl0", "xa", h, "zf")
    tolist(["xs"], "pl1", "xs", 1024, "zh")
    act(["n2", "lst%d" % r], ["of3"], T.of3[:, :], T.n2[:, :].indirect(T.lst[:, 36 * r:36 * r + 32]), bias=32.0)
    store(["of3"], T.yf[:, 68:580], T.of3[0:128:16, :], "a")
    fails_out(1)
    ts(["i3"], ["mx"], T.mx[:, :], T.i3[:, :], 32.0, A.add)
    tt(["pa0", "crt0", "crt1"], ["va"], T.va[:, :], T.pa0[:, 0:64], T.crt[:, :], A.is_gt)
    tt(["pa1", "mx"], ["mx"], T.mx[:, :], T.pa1[:, 0:64], T.mx[:, :], A.max)
    tt(["pa0", "va"], ["vb"], T.vb[:, :], T.pa0[:, 0:64], T.va[:, :], A.mult)
    for h in range(2):
        tt(["vb", "mx"], ["mx%d" % h], T.mx[:, 32 * h:32 * h + 32], T.vb[:, h:64:2], T.mx[:, 32 * h:32 * h + 32], A.max)
    for h in range(2):
        cp(["pl0"], ["oyl%d" % h], T.oyl[:, 32 * h:32 * h + 32], T.pl0[:, h:64:2])
    store(["oyl0", "oyl1"], T.yl[:, :], T.oyl[:, :])
    tt(["oyl0", "oyl1", "mx0", "mx1"], ["va"], T.va[:, :], T.oyl[:, :], T.mx[:, :], A.max)
    tt(["va", "pl1"], ["oym"], T.oym[:, :], T.pl1[:, 0:64], T.va[:, :], A.max)
    store(["oym"], T.ym[:, :], T.oym[:, :], "a")

    g.wait_ge(T.sem.snd, nsent[0])
    for e in ("v", "a", "p", "g"):
        need("y", (SEM[e], cnt[e], e, {}))
    g.sync.wait_ge(T.sem.out, nout[0])
